import numpy as np
import ml_dtypes


def mxq(x, axis, fmt="e4m3"):
    dtype, down = {"e4m3": (ml_dtypes.float8_e4m3fn, 7), "e5m2": (ml_dtypes.float8_e5m2, 14)}[fmt]
    v = np.moveaxis(np.asarray(x, np.float32).astype(ml_dtypes.bfloat16).astype(np.float64), axis, -1)
    blocks = v.reshape(v.shape[:-1] + (-1, 32))
    amax = np.abs(blocks).max(-1, keepdims=True)
    byte = np.maximum(np.where(amax > 0, np.frexp(amax)[1] - 1 + 127, 0) - down, 1)
    scale = np.exp2(byte - 127.0)
    codes = (blocks / scale).astype(np.float32).astype(dtype).astype(np.float64)
    return np.moveaxis((codes * scale).reshape(v.shape), -1, axis)


WIDE = False


def mx_kscale(k):
    if not WIDE:
        return np.ones(k)
    levels = np.array([10, -10, 5, -5, 0])
    if k % 512:
        return np.exp2(np.random.permutation(np.resize(levels, k // 32))).repeat(32)
    a = np.empty((k // 512, 16))
    for p in range(k // 512):
        a[p, :8] = np.random.permutation(np.resize(levels, 8))
        for g in range(8):
            far = levels[np.abs(levels - a[p, g]) >= 10]
            a[p, g + 8] = far[np.random.randint(len(far))]
    return np.exp2(a.ravel()).repeat(32)


BF16 = ml_dtypes.bfloat16


def bf(x):
    return np.asarray(x, np.float32).astype(BF16)


def f64(x):
    return np.asarray(x).astype(np.float64)


E2M1 = np.array([0.0, 0.5, 1.0, 1.5, 2.0, 3.0, 4.0, 6.0, -0.0, -0.5, -1.0, -1.5, -2.0, -3.0, -4.0, -6.0])


def pack_weight(w, fmt):
    k, n = w.shape
    w = f64(bf(w)).reshape(k // 32, 32, n)
    amax = np.abs(w).max(1)
    if fmt == "e4m3":
        byte = np.frexp(amax)[1] - 1 + 127 - 7
    else:
        mant, ex = np.frexp(amax / 6.0)
        byte = np.where(mant > 0.5, ex, ex - 1) + 127
    byte = np.clip(np.where(amax > 0, byte, 1), 1, 254)
    scaled = (w * np.exp2(127.0 - byte)[:, None, :]).reshape(k, n).astype(np.float32)
    by_word = np.ascontiguousarray(scaled.reshape(k // 512, 128, 4, n).transpose(0, 1, 3, 2))
    if fmt == "e4m3":
        words = by_word.astype(ml_dtypes.float8_e4m3fn).view(np.uint8)
    else:
        c = by_word.astype(ml_dtypes.float4_e2m1fn).view(np.uint8) & 0xF
        words = c[..., 0::2] | (c[..., 1::2] << 4)
    return np.ascontiguousarray(words), np.ascontiguousarray(byte.astype(np.uint8).reshape(k // 512, 16, n))


def unpack_weight(words, scales, fmt):
    g, p, n, _ = words.shape
    if fmt == "e4m3":
        vals = np.ascontiguousarray(words).view(ml_dtypes.float8_e4m3fn).astype(np.float64)
    else:
        nib = np.empty((g, p, n, 4), np.uint8)
        nib[..., 0::2] = words & 0xF
        nib[..., 1::2] = words >> 4
        vals = E2M1[nib]
    vals = vals * np.repeat(np.exp2(scales.astype(np.float64) - 127.0), 8, axis=1)[..., None]
    return vals.transpose(0, 1, 3, 2).reshape(g * 512, n)
def pack4(w):
    words, scales = pack_weight(w, "e2m1")
    return words.reshape(words.shape[0], 128, -1), scales


def unpack4(words, scales):
    return unpack_weight(words.reshape(words.shape[0], 128, -1, 2), scales, "e2m1")


M, T, N, L, P, Q = 1024, 2048, 1536, 512, 512, 4

HARD = 4.0
NOISE = 0.3


def setup_inputs():
    s, t, r = mx_kscale(T), mx_kscale(N), mx_kscale(L)
    src = np.random.standard_normal((T, Q))
    hu = np.random.standard_normal((Q, M))
    hv = np.random.standard_normal((Q, N))
    hu = hu / np.sqrt((hu ** 2).sum(0))
    hv = hv / np.sqrt((hv ** 2).sum(0))
    zu = (src[:, :, None] * hu[None]).sum(1) + NOISE * np.random.standard_normal((T, M))
    zv = (src[:, :, None] * hv[None]).sum(1) + NOISE * np.random.standard_normal((T, N))
    u_words, u_scales = pack4(np.tanh(HARD * zu) / np.sqrt(T) * s[:, None])
    v_words, v_scales = pack4(np.tanh(HARD * zv) * (np.pi / 2) / np.sqrt(T) / s[:, None])
    return {"u_words": u_words, "u_scales": u_scales,
            "v_words": v_words, "v_scales": v_scales,
            "d_row": bf(np.exp(0.3 * np.random.standard_normal(M))),
            "d_col": bf(np.exp(0.3 * np.random.standard_normal(N)) * t),
            "steer": bf(np.random.standard_normal((N, L)) / np.sqrt(N) * r / t[:, None]),
            "taper": bf(np.random.standard_normal((L, P)) / np.sqrt(L) / r[:, None])}


def reference(u_words, u_scales, v_words, v_scales, d_row, d_col, steer, taper):
    c = unpack4(u_words, u_scales).T @ unpack4(v_words, v_scales)
    cov = np.sin(c) * f64(d_col)
    beams = mxq(f64(steer), 1, "e4m3") @ mxq(f64(taper), 0, "e4m3")
    y = mxq(cov, 1, "e4m3") @ mxq(beams, 0, "e4m3")
    return y * f64(d_row)[:, None]

@@ -1,0 +1,371 @@
+import math
+from contextlib import ExitStack
+
+import concourse.mybir as mybir
+from concourse.masks import make_identity
+
+M, T, N, L, NB = 1024, 2048, 1536, 512, 512
+FLOPS = 2 * M * N * T + 2 * N * L * NB + 2 * M * N * NB
+
+F32 = mybir.dt.float32
+BF16 = mybir.dt.bfloat16
+I32 = mybir.dt.int32
+U32 = mybir.dt.uint32
+U8 = mybir.dt.uint8
+FP8X4 = mybir.dt.float8_e4m3fn_x4
+FP4X4 = mybir.dt.float4_e2m1fn_x4
+ACT = mybir.ActivationFunctionType
+ALU = mybir.AluOpType
+
+P = 128
+KP = T // 512
+G = N // 512
+CH = 256
+NCH = M // CH
+ROUND = 1.5 * 2.0 ** 23
+TURN = 2.0 * math.pi
+
+UNITS = [(g, c) for g in range(G) for c in (0, 1)] + [(g, c) for c in (2, 3) for g in range(G)]
+
+AHEAD = 1
+PLAG = 1
+SINE_FIRST = 1
+SIDE0 = 0
+PER_S = 2
+PER_B = 2
+QLAG = 1
+OUT0 = 0
+BEAMS_EARLY = 0
+TAPER = 0
+DEAL2 = 0
+VR = (3, 5, 7, 9)
+
+def tile_onebit_array_covariance_s12_kernel(
+        tc, u_words, u_scales, v_words, v_scales, d_row, d_col, steer, taper, out):
+    nc = tc.nc
+    with ExitStack() as ctx:
+        keep = ctx.enter_context(tc.tile_pool(name="keep", bufs=1))
+        work = ctx.enter_context(tc.tile_pool(name="work", bufs=3))
+        ps_c = ctx.enter_context(tc.psum_pool(name="ps_c", bufs=4))
+        ps_x = ctx.enter_context(tc.psum_pool(name="ps_x", bufs=3))
+        ps_d = ctx.enter_context(tc.psum_pool(name="ps_d", bufs=1))
+        ctx.enter_context(tc.manual_schedule())
+
+        def kept(name, shape, dtype):
+            return keep.tile(shape, dtype, name=name, align_bytes=64)
+
+        uw, vw = u_words.bitcast(I32), v_words.bitcast(I32)
+        us, vs = u_scales.bitcast(I32), v_scales.bitcast(I32)
+
+        u_first = [kept("u_codes%d" % c, [P, KP, 2 * CH], U8) for c in range(2)]
+        u_late = kept("u_late", [P, KP, 4 * CH], U8)
+        u_plane = [kept("u_plane%d" % h, [P, KP, 512], U8) for h in range(2)]
+        v_raw = [kept("v_raw%d" % g, [P, KP, 1024], U8) for g in range(G)]
+        v_rawplane = [kept("v_rawplane0", [P, KP, 512], U8), kept("v_rawplane1", [P, KP, 1024], U8)]
+        v_codes = [kept("v_codes%d" % g, [P, KP, 4, 256], U8) for g in range(G)]
+        v_plane = [kept("v_plane%d" % g, [P, KP, 4, 128], U8) for g in range(G)]
+        steer_raw = [kept("steer_raw%d" % g, [P, 2048], BF16) for g in range(G)]
+        steer_t = [kept("steer_t%d" % g, [P, 2048], BF16) for g in range(G)]
+        steer_codes = [kept("steer_codes%d" % g, [P, 512], U32) for g in range(G)]
+        steer_plane = [kept("steer_plane%d" % g, [P, 512], U8) for g in range(G)]
+        taper_raw = kept("taper_raw", [P, 4, NB], BF16)
+        taper_i = kept("taper_i", [P, NB, 4], BF16)
+        taper_codes = kept("taper_codes", [P, NB], U32)
+        taper_plane = kept("taper_plane", [P, NB], U8)
+        beams_i = [kept("beams_i%d" % g, [P, NB, 4], BF16) for g in range(G)]
+        beams_codes = [kept("beams_codes%d" % g, [P, NB], U32) for g in range(G)]
+        beams_plane = [kept("beams_plane%d" % g, [P, NB], U8) for g in range(G)]
+        cov_codes = {u: kept("cov_codes%d_%d" % u, [P, CH], U32) for u in UNITS}
+        cov_plane = {u: kept("cov_plane%d_%d" % u, [P, CH], U8) for u in UNITS}
+        d_rows = kept("d_rows", [P, G * P], BF16)
+        d_rows32 = kept("d_rows32", [P, G * P], F32)
+        row_gain = kept("row_gain", [P, 8], F32)
+        ident = kept("ident", [P, P], F32)
+        warm = kept("warm", [P, 2], F32)
+        gains = ps_d.tile([P, G, P], F32, name="gains")
+
+        def load_codes(dst, src, w0, w1):
+            nc.sync.dma_start(out=dst[:].bitcast(I32), in_=src[:, :, w0:w1].rearrange("k p w -> p k w"))
+
+        def load_plane(dst, src, w0, w1):
+            for q in range(4):
+                nc.sync.dma_start(out=dst[32 * q:32 * q + 4, :, :].bitcast(I32),
+                                  in_=src[:, 4 * q:4 * q + 4, w0:w1].rearrange("k r w -> r k w"))
+
+        def load_steer(g):
+            nc.sync.dma_start(out=steer_raw[g][:],
+                              in_=steer[512 * g:512 * (g + 1), :].rearrange("(p a) l -> p (a l)", a=4))
+
+        def deal_v(g):
+            nc.vector.tensor_copy(
+                out=v_codes[g][:].bitcast(I32).rearrange("p k t (q w) -> p k t q w", w=4),
+                in_=v_raw[g][:].bitcast(I32).rearrange("p k (q t w) -> p k t q w", t=4, w=4))
+            raw = v_rawplane[0][:] if g == 0 else v_rawplane[1][:, :, 512 * (g - 1):512 * g]
+            nc.vector.tensor_copy(
+                out=v_plane[g][:].bitcast(I32).rearrange("p k t (q w) -> p k t q w", w=2),
+                in_=raw.bitcast(I32).rearrange("p k (q t w) -> p k t q w", t=4, w=2))
+
+        banks, turns, whole, frac, sines, cov = {}, {}, {}, {}, {}, {}
+
+        def gram(r, pair):
+            g, c = UNITS[r]
+            h, c0 = divmod(c * CH, 512)
+            bank = ps_c.tile([P, 2, CH], F32, name="gram")
+            banks[r, pair] = bank
+            for e in range(2):
+                t = 2 * pair + e
+                for k in range(KP):
+                    nc.tensor.matmul_mx(
+                        out=bank[:, e, :],
+                        lhsT=v_codes[g][:, k, t, :].bitcast(FP4X4), lhsT_scale=v_plane[g][:, k, t, :],
+                        rhs=(u_late[:, k, 2 * c0:2 * (c0 + CH)] if h else u_first[c][:, k, :]).bitcast(FP4X4),
+                        rhs_scale=u_plane[h][:, k, c0:c0 + CH],
+                        start=(k == 0), stop=(k == KP - 1))
+
+        def to_turns(r, pair):
+            if pair == 0:
+                turns[r] = work.tile([P, 2, CH, 2], F32, name="turns", bufs=AHEAD + 2)
+            nc.scalar.activation(out=turns[r][:, pair, :, :], in_=banks[r, pair][:].rearrange("p e i -> p i e"),
+                                 func=ACT.Copy, scale=1.0 / TURN)
+
+        def round_turns(r, engine):
+            whole[r] = work.tile([P, 4 * CH], I32, name="whole", bufs=1)
+            engine.tensor_scalar(out=whole[r][:], in0=turns[r][:].rearrange("p a i e -> p (a i e)"),
+                                 scalar1=1.0, scalar2=ROUND, op0=ALU.mult, op1=ALU.add)
+
+        def reduce_turns(r):
+            frac[r] = work.tile([P, 4 * CH], F32, name="frac")
+            nc.vector.scalar_tensor_tensor(out=frac[r][:], in0=whole[r][:], scalar=ROUND,
+                                           in1=turns[r][:].rearrange("p a i e -> p (a i e)"),
+                                           op0=ALU.subtract, op1=ALU.subtract)
+
+        def sine(r, i0=0, i1=CH):
+            if i0 == 0:
+                sines[r] = work.tile([P, 2, CH, 2], F32, name="sines", bufs=4)
+            nc.scalar.activation(out=sines[r][:, :, i0:i1, :],
+                                 in_=frac[r][:].rearrange("p (a i e) -> p a i e", a=2, e=2)[:, :, i0:i1, :],
+                                 func=ACT.Sin, scale=-TURN)
+
+        def scale_cov(r, i0=0, i1=CH):
+            g = UNITS[r][0]
+            if i0 == 0:
+                cov[r] = work.tile([P, CH, 2, 2], BF16, name="cov", align_bytes=64)
+            gain = gains[:, g, 0:4].rearrange("p (o a e) -> p o a e", o=1, a=2)
+            nc.vector.tensor_tensor(out=cov[r][:, i0:i1], in0=sines[r][:, :, i0:i1, :].rearrange("p a i e -> p i a e"),
+                                    in1=gain.to_broadcast([P, i1 - i0, 2, 2]), op=ALU.mult)
+
+        def quantize_cov(r, i0=0, i1=CH):
+            u = UNITS[r]
+            nc.vector.quantize_mx(out=cov_codes[u][:, i0:i1].bitcast(FP8X4), scales=cov_plane[u][:, i0:i1],
+                                  in_=cov[r][:, i0:i1].rearrange("p i a e -> p (i a e)"))
+
+        xbank = {}
+
+        def turn_steer(g, half):
+            bank = ps_x.tile([P, 4, P], F32, name="xbank")
+            xbank["s", g, half] = bank
+            words = steer_raw[g][:].bitcast(F32)
+            for x in range(4):
+                a, u = 2 * half + x // 2, x % 2
+                nc.tensor.transpose(bank[:, x, :], words[:, 256 * a + u:256 * (a + 1):2], ident[:])
+
+        def copy_out(on_vector, out, in_):
+            if on_vector:
+                nc.vector.tensor_copy(out=out, in_=in_)
+            else:
+                nc.scalar.copy(out=out, in_=in_)
+
+        def copy_steer(g, half, on_vector):
+            dst = steer_t[g][:].bitcast(F32).rearrange("p (t q h a x) -> p a q t h x", t=4, q=16, h=2, a=2)
+            copy_out(on_vector, out=dst[:, half], in_=xbank["s", g, half][:].rearrange("p x (q t h) -> p q t h x", t=4, h=2))
+
+        def quantize_steer(g):
+            nc.vector.quantize_mx(out=steer_codes[g][:].bitcast(FP8X4), scales=steer_plane[g][:], in_=steer_t[g][:])
+
+        def beams(g, quarter):
+            bank = ps_x.tile([P, 4, P], F32, name="xbank")
+            xbank["b", g, quarter] = bank
+            cols = slice(P * quarter, P * (quarter + 1))
+            for t in range(4):
+                nc.tensor.matmul_mx(
+                    out=bank[:, t, :],
+                    lhsT=steer_codes[g][:, P * t:P * (t + 1)].bitcast(FP8X4),
+                    lhsT_scale=steer_plane[g][:, P * t:P * (t + 1)],
+                    rhs=taper_codes[:, cols].bitcast(FP8X4), rhs_scale=taper_plane[:, cols],
+                    start=True, stop=True)
+
+        def copy_beams(g, quarter, on_vector):
+            copy_out(on_vector, out=beams_i[g][:, P * quarter:P * (quarter + 1), :],
+                           in_=xbank["b", g, quarter][:].rearrange("p t b -> p b t"))
+
+        def quantize_beams(g):
+            nc.vector.quantize_mx(out=beams_codes[g][:].bitcast(FP8X4), scales=beams_plane[g][:],
+                                  in_=beams_i[g][:].rearrange("p b t -> p (b t)"))
+
+        def project(it, groups):
+            c, c0 = divmod(it * P, CH)
+            if groups[0] == 0:
+                xbank["o", it] = ps_x.tile([P, 4, P], F32, name="xbank")
+            acc = xbank["o", it][:].rearrange("p t b -> p (t b)")
+            for g in groups:
+                nc.tensor.matmul_mx(
+                    out=acc,
+                    lhsT=cov_codes[g, c][:, c0:c0 + P].bitcast(FP8X4), lhsT_scale=cov_plane[g, c][:, c0:c0 + P],
+                    rhs=beams_codes[g][:].bitcast(FP8X4), rhs_scale=beams_plane[g][:],
+                    start=(g == 0), stop=(g == G - 1))
+
+        def store(it, on_vector=False):
+            res = work.tile([P, NB], F32, name="res", bufs=8)
+            acc = xbank["o", it][:].rearrange("p t b -> p (t b)")
+            if on_vector:
+                nc.vector.tensor_scalar(out=res[:], in0=acc, scalar1=row_gain[:, it:it + 1], scalar2=None, op0=ALU.mult)
+            else:
+                nc.scalar.activation(out=res[:], in_=acc, func=ACT.Copy, scale=row_gain[:, it:it + 1])
+            nc.sync.dma_start(out=out[P * it:P * (it + 1), :], in_=res[:])
+
+        def turn_gains():
+            for g in range(G):
+                nc.tensor.transpose(gains[:, g, :], d_rows32[:, P * g:P * (g + 1)], ident[:])
+
+        def load_gains():
+            nc.sync.dma_start(out=d_rows[0:4, :].rearrange("t (q r) -> t q r", r=8),
+                              in_=d_col.rearrange("(q t r) -> t q r", t=4, r=8))
+            nc.sync.dma_start(out=d_rows[16:24, 0:P], in_=d_row.rearrange("(a p) -> a p", p=P))
+
+        def taper_in():
+            nc.vector.tensor_copy(out=taper_i[:].rearrange("p (c i) t -> p c t i", i=4),
+                                  in_=taper_raw[:].rearrange("p t (c i) -> p c t i", i=4))
+
+        def quantize_taper():
+            nc.vector.quantize_mx(out=taper_codes[:].bitcast(FP8X4), scales=taper_plane[:],
+                                  in_=taper_i[:].rearrange("p b t -> p (b t)"))
+
+        nc.vector.memset(v_rawplane[0][:].bitcast(I32), 0)
+        nc.vector.memset(u_plane[0][:].bitcast(I32), 0)
+        nc.vector.memset(warm[:, 0:1], 0.0)
+        nc.scalar.activation(out=warm[:, 1:2], in_=warm[:, 0:1], func=ACT.Sin)
+        nc.vector.memset(d_rows[:], 0.0)
+        nc.vector.memset(v_rawplane[1][:].bitcast(I32), 0)
+        nc.vector.memset(u_plane[1][:].bitcast(I32), 0)
+        make_identity(nc, ident[:])
+
+        load_codes(v_raw[0], vw, 0, 256)
+        load_codes(u_first[0], uw, 0, 128)
+        load_plane(v_rawplane[0], vs, 0, 128)
+        load_plane(u_plane[0], us, 0, 128)
+        load_codes(u_first[1], uw, 128, 256)
+        load_gains()
+        load_codes(v_raw[1], vw, 256, 512)
+        load_plane(v_rawplane[1], vs, 128, 384)
+        nc.sync.dma_start(out=taper_raw[:], in_=taper.rearrange("(p t) b -> p t b", t=4))
+        load_steer(0)
+        load_steer(1)
+        load_codes(v_raw[2], vw, 512, 768)
+        load_steer(2)
+        load_codes(u_late, uw, 256, 512)
+        load_plane(u_plane[1], us, 128, 256)
+
+        nu = len(UNITS)
+        jobs = [("s", g, h) for g in range(G) for h in range(2)] + [("b", g, q) for g in range(G) for q in range(4)]
+        if BEAMS_EARLY:
+            jobs = jobs[0:4] + jobs[6:10] + jobs[4:6] + jobs[10:]
+        side = {}
+        at = {}
+        r = SIDE0
+        while jobs:
+            n = PER_S if jobs[0][0] == "s" else PER_B
+            side[r], jobs = jobs[:n], jobs[n:]
+            for j in side[r]:
+                at[j] = r
+            r = r + 1
+        vec = {}
+        for g in range(G):
+            vec.setdefault(at["s", g, 1] + QLAG, []).append(lambda g=g: quantize_steer(g))
+            vec.setdefault(at["b", g, 3] + QLAG, []).append(lambda g=g: quantize_beams(g))
+        r = max(at["b", G - 1, 3] + QLAG + 1, OUT0)
+        for c in range(3):
+            r = max(r, UNITS.index((G - 1, c)) + PLAG + 1)
+            side.setdefault(r, []).extend([("o", 2 * c), ("o", 2 * c + 1)])
+            r = r + 1
+        vec.setdefault(TAPER, []).extend([taper_in])
+        vec.setdefault(TAPER + 1, []).extend([quantize_taper])
+        vec.setdefault(DEAL2, []).append(lambda: deal_v(2))
+        vec.setdefault(3, []).append(lambda: nc.vector.tensor_copy(out=row_gain[:], in_=gains[:, 0, 16:24]))
+
+        def side_tensor(r):
+            for item in side.get(r, []):
+                if item[0] == "s":
+                    turn_steer(item[1], item[2])
+                elif item[0] == "b":
+                    beams(item[1], item[2])
+                else:
+                    project(item[1], list(range(G)))
+
+        def side_copies(r, on_vector):
+            items = side.get(r, [])
+            for item in items:
+                if (r in VR and item == items[-1] and item[0] != "s") != on_vector:
+                    continue
+                if item[0] == "s":
+                    copy_steer(item[1], item[2], on_vector)
+                elif item[0] == "b":
+                    copy_beams(item[1], item[2], on_vector)
+                else:
+                    store(item[1], on_vector)
+
+        deal_v(0)
+        for pair in range(2):
+            gram(0, pair)
+            to_turns(0, pair)
+        nc.vector.tensor_copy(out=d_rows32[:], in_=d_rows[:])
+        deal_v(1)
+        for call in vec.get(-1, []):
+            call()
+        round_turns(0, nc.vector)
+        for r in range(1, AHEAD):
+            for pair in range(2):
+                gram(r, pair)
+                to_turns(r, pair)
+        last = nu - 1
+        for r in range(nu + PLAG - 1):
+            if r + AHEAD < nu:
+                gram(r + AHEAD, 0)
+                gram(r + AHEAD, 1)
+            if r == 0:
+                turn_gains()
+            side_tensor(r)
+            if SINE_FIRST and 1 <= r <= last:
+                sine(r - 1)
+            if r + AHEAD < nu:
+                to_turns(r + AHEAD, 0)
+                to_turns(r + AHEAD, 1)
+            if not SINE_FIRST and 1 <= r <= last:
+                sine(r - 1)
+            if r < nu:
+                reduce_turns(r)
+            if r + 1 < nu:
+                round_turns(r + 1, nc.gpsimd)
+            if r >= PLAG:
+                scale_cov(r - PLAG)
+            side_copies(r, True)
+            if r >= PLAG:
+                quantize_cov(r - PLAG)
+            if r == last:
+                for half in range(2):
+                    sine(last, P * half, P * (half + 1))
+            side_copies(r, False)
+            for call in vec.get(r, []):
+                call()
+        for r in range(nu + PLAG - 1, nu + 4):
+            side_tensor(r)
+            side_copies(r, True)
+            side_copies(r, False)
+        for half in range(2):
+            project(6 + half, [0, 1])
+        for half in range(2):
+            scale_cov(last, P * half, P * (half + 1))
+        for half in range(2):
+            quantize_cov(last, P * half, P * (half + 1))
+            project(6 + half, [2])
+        store(6)
+        store(7, on_vector=True)

@@ -30,15 +30,17 @@ UNITS = [(g, c) for g in range(G) for c in (0, 1)] + [(g, c) for c in (2, 3) for
 AHEAD = 1
 PLAG = 1
 SINE_FIRST = 1
-SIDE0 = 0
+SIDE0 = 1
 PER_S = 2
 PER_B = 2
-QLAG = 1
+QLAG = 0
 OUT0 = 0
-BEAMS_EARLY = 0
-TAPER = 0
+BEAMS_EARLY = 1
 DEAL2 = 0
-VR = (3, 5, 7, 9)
+VR = ()
+SC = 0
+CB = 4
+ORDER = "tud1p2abcUP"
 
 def tile_onebit_array_covariance_s12_kernel(
         tc, u_words, u_scales, v_words, v_scales, d_row, d_col, steer, taper, out):
@@ -46,9 +48,8 @@ def tile_onebit_array_covariance_s12_kernel(
     with ExitStack() as ctx:
         keep = ctx.enter_context(tc.tile_pool(name="keep", bufs=1))
         work = ctx.enter_context(tc.tile_pool(name="work", bufs=3))
-        ps_c = ctx.enter_context(tc.psum_pool(name="ps_c", bufs=4))
-        ps_x = ctx.enter_context(tc.psum_pool(name="ps_x", bufs=3))
-        ps_d = ctx.enter_context(tc.psum_pool(name="ps_d", bufs=1))
+        ps_c = ctx.enter_context(tc.psum_pool(name="ps_c", bufs=CB))
+        ps_x = ctx.enter_context(tc.psum_pool(name="ps_x", bufs=8 - CB))
         ctx.enter_context(tc.manual_schedule())
 
         def kept(name, shape, dtype):
@@ -79,16 +80,15 @@ def tile_onebit_array_covariance_s12_kernel(
         cov_plane = {u: kept("cov_plane%d_%d" % u, [P, CH], U8) for u in UNITS}
         d_rows = kept("d_rows", [P, G * P], BF16)
         d_rows32 = kept("d_rows32", [P, G * P], F32)
-        row_gain = kept("row_gain", [P, 8], F32)
         ident = kept("ident", [P, P], F32)
         warm = kept("warm", [P, 2], F32)
-        gains = ps_d.tile([P, G, P], F32, name="gains")
+        gains = kept("gains", [P, G, 24], F32)
 
         def load_codes(dst, src, w0, w1):
             nc.sync.dma_start(out=dst[:].bitcast(I32), in_=src[:, :, w0:w1].rearrange("k p w -> p k w"))
 
-        def load_plane(dst, src, w0, w1):
-            for q in range(4):
+        def load_plane(dst, src, w0, w1, quadrants=range(4)):
+            for q in quadrants:
                 nc.sync.dma_start(out=dst[32 * q:32 * q + 4, :, :].bitcast(I32),
                                   in_=src[:, 4 * q:4 * q + 4, w0:w1].rearrange("k r w -> r k w"))
 
@@ -127,11 +127,17 @@ def tile_onebit_array_covariance_s12_kernel(
                 turns[r] = work.tile([P, 2, CH, 2], F32, name="turns", bufs=AHEAD + 2)
             nc.scalar.activation(out=turns[r][:, pair, :, :], in_=banks[r, pair][:].rearrange("p e i -> p i e"),
                                  func=ACT.Copy, scale=1.0 / TURN)
+            if pair == 0:
+                whole[r] = work.tile([P, 4 * CH], I32, name="whole", bufs=AHEAD + 2)
+                if SC:
+                    nc.scalar.activation(out=whole[r][:, 0:SC].bitcast(U32).rearrange("p (i e) -> p i e", e=2),
+                                         in_=banks[r, 0][:].rearrange("p e i -> p i e")[:, 0:SC // 2, :],
+                                         func=ACT.Copy, scale=1.0 / TURN, bias=ROUND)
 
-        def round_turns(r, engine):
-            whole[r] = work.tile([P, 4 * CH], I32, name="whole", bufs=1)
-            engine.tensor_scalar(out=whole[r][:], in0=turns[r][:].rearrange("p a i e -> p (a i e)"),
-                                 scalar1=1.0, scalar2=ROUND, op0=ALU.mult, op1=ALU.add)
+        def round_turns(r):
+            nc.vector.tensor_scalar(out=whole[r][:, SC:],
+                                    in0=turns[r][:].rearrange("p a i e -> p (a i e)")[:, SC:],
+                                    scalar1=ROUND, scalar2=None, op0=ALU.add)
 
         def reduce_turns(r):
             frac[r] = work.tile([P, 4 * CH], F32, name="frac")
@@ -218,14 +224,19 @@ def tile_onebit_array_covariance_s12_kernel(
             res = work.tile([P, NB], F32, name="res", bufs=8)
             acc = xbank["o", it][:].rearrange("p t b -> p (t b)")
             if on_vector:
-                nc.vector.tensor_scalar(out=res[:], in0=acc, scalar1=row_gain[:, it:it + 1], scalar2=None, op0=ALU.mult)
+                nc.vector.tensor_scalar(out=res[:], in0=acc, scalar1=gains[:, 0, 16 + it:17 + it], scalar2=None, op0=ALU.mult)
             else:
-                nc.scalar.activation(out=res[:], in_=acc, func=ACT.Copy, scale=row_gain[:, it:it + 1])
+                nc.scalar.activation(out=res[:], in_=acc, func=ACT.Copy, scale=gains[:, 0, 16 + it:17 + it])
             nc.sync.dma_start(out=out[P * it:P * (it + 1), :], in_=res[:])
 
         def turn_gains():
+            bank = ps_x.tile([P, 4, P], F32, name="xbank")
             for g in range(G):
-                nc.tensor.transpose(gains[:, g, :], d_rows32[:, P * g:P * (g + 1)], ident[:])
+                nc.tensor.transpose(bank[:, g, :], d_rows32[:, P * g:P * (g + 1)], ident[:])
+            xbank["gains"] = bank
+
+        def copy_gains():
+            nc.scalar.copy(out=gains[:], in_=xbank["gains"][:, 0:G, 0:24])
 
         def load_gains():
             nc.sync.dma_start(out=d_rows[0:4, :].rearrange("t (q r) -> t q r", r=8),
@@ -249,22 +260,24 @@ def tile_onebit_array_covariance_s12_kernel(
         nc.vector.memset(u_plane[1][:].bitcast(I32), 0)
         make_identity(nc, ident[:])
 
-        load_codes(v_raw[0], vw, 0, 256)
         load_codes(u_first[0], uw, 0, 128)
-        load_plane(v_rawplane[0], vs, 0, 128)
+        load_plane(v_rawplane[0], vs, 0, 128, range(1))
+        load_codes(v_raw[0], vw, 0, 256)
+        load_plane(v_rawplane[0], vs, 0, 128, range(1, 4))
         load_plane(u_plane[0], us, 0, 128)
-        load_codes(u_first[1], uw, 128, 256)
-        load_gains()
-        load_codes(v_raw[1], vw, 256, 512)
-        load_plane(v_rawplane[1], vs, 128, 384)
-        nc.sync.dma_start(out=taper_raw[:], in_=taper.rearrange("(p t) b -> p t b", t=4))
-        load_steer(0)
-        load_steer(1)
-        load_codes(v_raw[2], vw, 512, 768)
-        load_steer(2)
-        load_codes(u_late, uw, 256, 512)
-        load_plane(u_plane[1], us, 128, 256)
-
+        loads = {
+            "u": lambda: load_codes(u_first[1], uw, 128, 256),
+            "d": load_gains,
+            "1": lambda: load_codes(v_raw[1], vw, 256, 512),
+            "p": lambda: load_plane(v_rawplane[1], vs, 128, 384),
+            "t": lambda: nc.sync.dma_start(out=taper_raw[:], in_=taper.rearrange("(p t) b -> p t b", t=4)),
+            "2": lambda: load_codes(v_raw[2], vw, 512, 768),
+            "a": lambda: load_steer(0), "b": lambda: load_steer(1), "c": lambda: load_steer(2),
+            "U": lambda: load_codes(u_late, uw, 256, 512),
+            "P": lambda: load_plane(u_plane[1], us, 128, 256),
+        }
+        for key in ORDER:
+            loads[key]()
         nu = len(UNITS)
         jobs = [("s", g, h) for g in range(G) for h in range(2)] + [("b", g, q) for g in range(G) for q in range(4)]
         if BEAMS_EARLY:
@@ -287,10 +300,7 @@ def tile_onebit_array_covariance_s12_kernel(
             r = max(r, UNITS.index((G - 1, c)) + PLAG + 1)
             side.setdefault(r, []).extend([("o", 2 * c), ("o", 2 * c + 1)])
             r = r + 1
-        vec.setdefault(TAPER, []).extend([taper_in])
-        vec.setdefault(TAPER + 1, []).extend([quantize_taper])
         vec.setdefault(DEAL2, []).append(lambda: deal_v(2))
-        vec.setdefault(3, []).append(lambda: nc.vector.tensor_copy(out=row_gain[:], in_=gains[:, 0, 16:24]))
 
         def side_tensor(r):
             for item in side.get(r, []):
@@ -317,11 +327,13 @@ def tile_onebit_array_covariance_s12_kernel(
         for pair in range(2):
             gram(0, pair)
             to_turns(0, pair)
+        taper_in()
         nc.vector.tensor_copy(out=d_rows32[:], in_=d_rows[:])
+        quantize_taper()
         deal_v(1)
         for call in vec.get(-1, []):
             call()
-        round_turns(0, nc.vector)
+        round_turns(0)
         for r in range(1, AHEAD):
             for pair in range(2):
                 gram(r, pair)
@@ -339,21 +351,23 @@ def tile_onebit_array_covariance_s12_kernel(
             if r + AHEAD < nu:
                 to_turns(r + AHEAD, 0)
                 to_turns(r + AHEAD, 1)
+            if r == 0:
+                copy_gains()
             if not SINE_FIRST and 1 <= r <= last:
                 sine(r - 1)
             if r < nu:
                 reduce_turns(r)
-            if r + 1 < nu:
-                round_turns(r + 1, nc.gpsimd)
             if r >= PLAG:
                 scale_cov(r - PLAG)
             side_copies(r, True)
+            if r + 1 < nu:
+                round_turns(r + 1)
             if r >= PLAG:
                 quantize_cov(r - PLAG)
+            side_copies(r, False)
             if r == last:
                 for half in range(2):
                     sine(last, P * half, P * (half + 1))
-            side_copies(r, False)
             for call in vec.get(r, []):
                 call()
         for r in range(nu + PLAG - 1, nu + 4):

@@ -18,29 +18,17 @@ ACT = mybir.ActivationFunctionType
 ALU = mybir.AluOpType
 
 P = 128
-KP = T // 512
-G = N // 512
-CH = 256
-NCH = M // CH
-ROUND = 1.5 * 2.0 ** 23
+PASSES = T // 512
+GROUPS = N // 512
+CHUNK = 256
+COLS = 4 * CHUNK
 TURN = 2.0 * math.pi
+ROUND = 1.5 * 2.0 ** 23
+GPSIMD_COLS = 640
+GAIN_ROW = 16
 
-UNITS = [(g, c) for g in range(G) for c in (0, 1)] + [(g, c) for c in (2, 3) for g in range(G)]
+UNITS = [(g, c) for g in range(GROUPS) for c in (0, 1)] + [(g, c) for c in (2, 3) for g in range(GROUPS)]
 
-AHEAD = 1
-PLAG = 1
-SINE_FIRST = 1
-SIDE0 = 1
-PER_S = 2
-PER_B = 2
-QLAG = 0
-OUT0 = 0
-BEAMS_EARLY = 1
-DEAL2 = 0
-VR = ()
-SC = 0
-CB = 4
-ORDER = "tud1p2abcUP"
 
 def tile_onebit_array_covariance_s12_kernel(
         tc, u_words, u_scales, v_words, v_scales, d_row, d_col, steer, taper, out):
@@ -48,8 +36,9 @@ def tile_onebit_array_covariance_s12_kernel(
     with ExitStack() as ctx:
         keep = ctx.enter_context(tc.tile_pool(name="keep", bufs=1))
         work = ctx.enter_context(tc.tile_pool(name="work", bufs=3))
-        ps_c = ctx.enter_context(tc.psum_pool(name="ps_c", bufs=CB))
-        ps_x = ctx.enter_context(tc.psum_pool(name="ps_x", bufs=8 - CB))
+        gram_banks = ctx.enter_context(tc.psum_pool(name="gram_banks", bufs=4))
+        side_banks = ctx.enter_context(tc.psum_pool(name="side_banks", bufs=3))
+        gain_bank = ctx.enter_context(tc.psum_pool(name="gain_bank", bufs=1))
         ctx.enter_context(tc.manual_schedule())
 
         def kept(name, shape, dtype):
@@ -58,31 +47,34 @@ def tile_onebit_array_covariance_s12_kernel(
         uw, vw = u_words.bitcast(I32), v_words.bitcast(I32)
         us, vs = u_scales.bitcast(I32), v_scales.bitcast(I32)
 
-        u_first = [kept("u_codes%d" % c, [P, KP, 2 * CH], U8) for c in range(2)]
-        u_late = kept("u_late", [P, KP, 4 * CH], U8)
-        u_plane = [kept("u_plane%d" % h, [P, KP, 512], U8) for h in range(2)]
-        v_raw = [kept("v_raw%d" % g, [P, KP, 1024], U8) for g in range(G)]
-        v_rawplane = [kept("v_rawplane0", [P, KP, 512], U8), kept("v_rawplane1", [P, KP, 1024], U8)]
-        v_codes = [kept("v_codes%d" % g, [P, KP, 4, 256], U8) for g in range(G)]
-        v_plane = [kept("v_plane%d" % g, [P, KP, 4, 128], U8) for g in range(G)]
-        steer_raw = [kept("steer_raw%d" % g, [P, 2048], BF16) for g in range(G)]
-        steer_t = [kept("steer_t%d" % g, [P, 2048], BF16) for g in range(G)]
-        steer_codes = [kept("steer_codes%d" % g, [P, 512], U32) for g in range(G)]
-        steer_plane = [kept("steer_plane%d" % g, [P, 512], U8) for g in range(G)]
+        u_first = [kept("u_codes%d" % c, [P, PASSES, 2 * CHUNK], U8) for c in range(2)]
+        u_late = kept("u_late", [P, PASSES, 4 * CHUNK], U8)
+        u_plane = [kept("u_plane%d" % h, [P, PASSES, 2 * CHUNK], U8) for h in range(2)]
+        v_raw = [kept("v_raw%d" % g, [P, PASSES, 1024], U8) for g in range(GROUPS)]
+        v_rawplane = [kept("v_rawplane0", [P, PASSES, 512], U8),
+                      kept("v_rawplane1", [P, PASSES, 1024], U8)]
+        v_codes = [kept("v_codes%d" % g, [P, PASSES, 4, 2 * P], U8) for g in range(GROUPS)]
+        v_plane = [kept("v_plane%d" % g, [P, PASSES, 4, P], U8) for g in range(GROUPS)]
+        steer_raw = [kept("steer_raw%d" % g, [P, 4 * L], BF16) for g in range(GROUPS)]
+        steer_t = [kept("steer_t%d" % g, [P, 4 * 512], BF16) for g in range(GROUPS)]
+        steer_codes = [kept("steer_codes%d" % g, [P, 512], U32) for g in range(GROUPS)]
+        steer_plane = [kept("steer_plane%d" % g, [P, 512], U8) for g in range(GROUPS)]
         taper_raw = kept("taper_raw", [P, 4, NB], BF16)
         taper_i = kept("taper_i", [P, NB, 4], BF16)
         taper_codes = kept("taper_codes", [P, NB], U32)
         taper_plane = kept("taper_plane", [P, NB], U8)
-        beams_i = [kept("beams_i%d" % g, [P, NB, 4], BF16) for g in range(G)]
-        beams_codes = [kept("beams_codes%d" % g, [P, NB], U32) for g in range(G)]
-        beams_plane = [kept("beams_plane%d" % g, [P, NB], U8) for g in range(G)]
-        cov_codes = {u: kept("cov_codes%d_%d" % u, [P, CH], U32) for u in UNITS}
-        cov_plane = {u: kept("cov_plane%d_%d" % u, [P, CH], U8) for u in UNITS}
-        d_rows = kept("d_rows", [P, G * P], BF16)
-        d_rows32 = kept("d_rows32", [P, G * P], F32)
+        beams_i = [kept("beams_i%d" % g, [P, NB, 4], BF16) for g in range(GROUPS)]
+        beams_codes = [kept("beams_codes%d" % g, [P, NB], U32) for g in range(GROUPS)]
+        beams_plane = [kept("beams_plane%d" % g, [P, NB], U8) for g in range(GROUPS)]
+        cov_codes = {unit: kept("cov_codes%d_%d" % unit, [P, CHUNK], U32) for unit in UNITS}
+        cov_plane = {unit: kept("cov_plane%d_%d" % unit, [P, CHUNK], U8) for unit in UNITS}
+        d_rows = kept("d_rows", [P, GROUPS * P], BF16)
+        d_rows32 = kept("d_rows32", [P, GROUPS * P], F32)
         ident = kept("ident", [P, P], F32)
         warm = kept("warm", [P, 2], F32)
-        gains = kept("gains", [P, G, 24], F32)
+        gains = gain_bank.tile([P, GROUPS, P], F32, name="gains")
+        row_gain = kept("row_gain", [P, M // P], F32)
+
 
         def load_codes(dst, src, w0, w1):
             nc.sync.dma_start(out=dst[:].bitcast(I32), in_=src[:, :, w0:w1].rearrange("k p w -> p k w"))
@@ -94,7 +86,13 @@ def tile_onebit_array_covariance_s12_kernel(
 
         def load_steer(g):
             nc.sync.dma_start(out=steer_raw[g][:],
-                              in_=steer[512 * g:512 * (g + 1), :].rearrange("(p a) l -> p (a l)", a=4))
+                              in_=steer[512 * g:512 * (g + 1), :].rearrange("(s a) l -> s (a l)", a=4))
+
+        def load_gains():
+            nc.sync.dma_start(out=d_rows[0:4, :].rearrange("t (q r) -> t q r", r=8),
+                              in_=d_col.rearrange("(q t r) -> t q r", t=4, r=8))
+            nc.sync.dma_start(out=d_rows[GAIN_ROW:GAIN_ROW + M // P, 0:P], in_=d_row.rearrange("(a p) -> a p", p=P))
+
 
         def deal_v(g):
             nc.vector.tensor_copy(
@@ -105,92 +103,96 @@ def tile_onebit_array_covariance_s12_kernel(
                 out=v_plane[g][:].bitcast(I32).rearrange("p k t (q w) -> p k t q w", w=2),
                 in_=raw.bitcast(I32).rearrange("p k (q t w) -> p k t q w", t=4, w=2))
 
+        def interleave_taper():
+            nc.vector.tensor_copy(out=taper_i[:].rearrange("p (c i) t -> p c t i", i=4),
+                                  in_=taper_raw[:].rearrange("p t (c i) -> p c t i", i=4))
+
+        def quantize(codes, plane, values):
+            nc.vector.quantize_mx(out=codes.bitcast(FP8X4), scales=plane, in_=values)
+
+        def turn_gains():
+            for g in range(GROUPS):
+                nc.tensor.transpose(gains[:, g, :], d_rows32[:, P * g:P * (g + 1)], ident[:])
+
+
         banks, turns, whole, frac, sines, cov = {}, {}, {}, {}, {}, {}
 
         def gram(r, pair):
             g, c = UNITS[r]
-            h, c0 = divmod(c * CH, 512)
-            bank = ps_c.tile([P, 2, CH], F32, name="gram")
+            h, i0 = divmod(c * CHUNK, 2 * CHUNK)
+            bank = gram_banks.tile([P, 2, CHUNK], F32, name="gram")
             banks[r, pair] = bank
             for e in range(2):
                 t = 2 * pair + e
-                for k in range(KP):
+                for k in range(PASSES):
+                    rows = u_late[:, k, 2 * i0:2 * (i0 + CHUNK)] if h else u_first[c][:, k, :]
                     nc.tensor.matmul_mx(
                         out=bank[:, e, :],
                         lhsT=v_codes[g][:, k, t, :].bitcast(FP4X4), lhsT_scale=v_plane[g][:, k, t, :],
-                        rhs=(u_late[:, k, 2 * c0:2 * (c0 + CH)] if h else u_first[c][:, k, :]).bitcast(FP4X4),
-                        rhs_scale=u_plane[h][:, k, c0:c0 + CH],
-                        start=(k == 0), stop=(k == KP - 1))
+                        rhs=rows.bitcast(FP4X4), rhs_scale=u_plane[h][:, k, i0:i0 + CHUNK],
+                        start=(k == 0), stop=(k == PASSES - 1))
 
         def to_turns(r, pair):
             if pair == 0:
-                turns[r] = work.tile([P, 2, CH, 2], F32, name="turns", bufs=AHEAD + 2)
+                turns[r] = work.tile([P, 2, CHUNK, 2], F32, name="turns")
             nc.scalar.activation(out=turns[r][:, pair, :, :], in_=banks[r, pair][:].rearrange("p e i -> p i e"),
                                  func=ACT.Copy, scale=1.0 / TURN)
-            if pair == 0:
-                whole[r] = work.tile([P, 4 * CH], I32, name="whole", bufs=AHEAD + 2)
-                if SC:
-                    nc.scalar.activation(out=whole[r][:, 0:SC].bitcast(U32).rearrange("p (i e) -> p i e", e=2),
-                                         in_=banks[r, 0][:].rearrange("p e i -> p i e")[:, 0:SC // 2, :],
-                                         func=ACT.Copy, scale=1.0 / TURN, bias=ROUND)
 
-        def round_turns(r):
-            nc.vector.tensor_scalar(out=whole[r][:, SC:],
-                                    in0=turns[r][:].rearrange("p a i e -> p (a i e)")[:, SC:],
-                                    scalar1=ROUND, scalar2=None, op0=ALU.add)
+        def new_whole(r):
+            whole[r] = work.tile([P, COLS], I32, name="whole", bufs=1)
+
+        def round_turns(r, engine, c0, c1):
+            engine.tensor_scalar(out=whole[r][:, c0:c1],
+                                 in0=turns[r][:].rearrange("p a i e -> p (a i e)")[:, c0:c1],
+                                 scalar1=1.0, scalar2=ROUND, op0=ALU.mult, op1=ALU.add)
 
         def reduce_turns(r):
-            frac[r] = work.tile([P, 4 * CH], F32, name="frac")
+            frac[r] = work.tile([P, COLS], F32, name="frac")
             nc.vector.scalar_tensor_tensor(out=frac[r][:], in0=whole[r][:], scalar=ROUND,
                                            in1=turns[r][:].rearrange("p a i e -> p (a i e)"),
                                            op0=ALU.subtract, op1=ALU.subtract)
 
-        def sine(r, i0=0, i1=CH):
+        def sine(r, i0=0, i1=CHUNK):
             if i0 == 0:
-                sines[r] = work.tile([P, 2, CH, 2], F32, name="sines", bufs=4)
+                sines[r] = work.tile([P, 2, CHUNK, 2], F32, name="sines", bufs=4)
             nc.scalar.activation(out=sines[r][:, :, i0:i1, :],
                                  in_=frac[r][:].rearrange("p (a i e) -> p a i e", a=2, e=2)[:, :, i0:i1, :],
                                  func=ACT.Sin, scale=-TURN)
 
-        def scale_cov(r, i0=0, i1=CH):
+        def scale_cov(r, i0=0, i1=CHUNK):
             g = UNITS[r][0]
             if i0 == 0:
-                cov[r] = work.tile([P, CH, 2, 2], BF16, name="cov", align_bytes=64)
+                cov[r] = work.tile([P, CHUNK, 2, 2], BF16, name="cov", align_bytes=64)
             gain = gains[:, g, 0:4].rearrange("p (o a e) -> p o a e", o=1, a=2)
-            nc.vector.tensor_tensor(out=cov[r][:, i0:i1], in0=sines[r][:, :, i0:i1, :].rearrange("p a i e -> p i a e"),
+            nc.vector.tensor_tensor(out=cov[r][:, i0:i1],
+                                    in0=sines[r][:, :, i0:i1, :].rearrange("p a i e -> p i a e"),
                                     in1=gain.to_broadcast([P, i1 - i0, 2, 2]), op=ALU.mult)
 
-        def quantize_cov(r, i0=0, i1=CH):
-            u = UNITS[r]
-            nc.vector.quantize_mx(out=cov_codes[u][:, i0:i1].bitcast(FP8X4), scales=cov_plane[u][:, i0:i1],
-                                  in_=cov[r][:, i0:i1].rearrange("p i a e -> p (i a e)"))
+        def quantize_cov(r, i0=0, i1=CHUNK):
+            quantize(cov_codes[UNITS[r]][:, i0:i1], cov_plane[UNITS[r]][:, i0:i1],
+                     cov[r][:, i0:i1].rearrange("p i a e -> p (i a e)"))
 
-        xbank = {}
+
+        side_bank = {}
+
+        def new_side_bank(job):
+            side_bank[job] = side_banks.tile([P, 4, P], F32, name="side_bank")
+            return side_bank[job]
 
         def turn_steer(g, half):
-            bank = ps_x.tile([P, 4, P], F32, name="xbank")
-            xbank["s", g, half] = bank
+            bank = new_side_bank(("steer", g, half))
             words = steer_raw[g][:].bitcast(F32)
             for x in range(4):
                 a, u = 2 * half + x // 2, x % 2
                 nc.tensor.transpose(bank[:, x, :], words[:, 256 * a + u:256 * (a + 1):2], ident[:])
 
-        def copy_out(on_vector, out, in_):
-            if on_vector:
-                nc.vector.tensor_copy(out=out, in_=in_)
-            else:
-                nc.scalar.copy(out=out, in_=in_)
-
-        def copy_steer(g, half, on_vector):
-            dst = steer_t[g][:].bitcast(F32).rearrange("p (t q h a x) -> p a q t h x", t=4, q=16, h=2, a=2)
-            copy_out(on_vector, out=dst[:, half], in_=xbank["s", g, half][:].rearrange("p x (q t h) -> p q t h x", t=4, h=2))
-
-        def quantize_steer(g):
-            nc.vector.quantize_mx(out=steer_codes[g][:].bitcast(FP8X4), scales=steer_plane[g][:], in_=steer_t[g][:])
+        def copy_steer(g, half):
+            dst = steer_t[g][:].bitcast(F32).rearrange("p (t q h f x) -> p f q t h x", t=4, q=16, h=2, f=2)
+            nc.scalar.copy(out=dst[:, half],
+                           in_=side_bank["steer", g, half][:].rearrange("p x (q t h) -> p q t h x", t=4, h=2))
 
         def beams(g, quarter):
-            bank = ps_x.tile([P, 4, P], F32, name="xbank")
-            xbank["b", g, quarter] = bank
+            bank = new_side_bank(("beams", g, quarter))
             cols = slice(P * quarter, P * (quarter + 1))
             for t in range(4):
                 nc.tensor.matmul_mx(
@@ -200,56 +202,76 @@ def tile_onebit_array_covariance_s12_kernel(
                     rhs=taper_codes[:, cols].bitcast(FP8X4), rhs_scale=taper_plane[:, cols],
                     start=True, stop=True)
 
-        def copy_beams(g, quarter, on_vector):
-            copy_out(on_vector, out=beams_i[g][:, P * quarter:P * (quarter + 1), :],
-                           in_=xbank["b", g, quarter][:].rearrange("p t b -> p b t"))
+        def copy_beams(g, quarter, copy):
+            copy(out=beams_i[g][:, P * quarter:P * (quarter + 1), :],
+                 in_=side_bank["beams", g, quarter][:].rearrange("p t b -> p b t"))
 
-        def quantize_beams(g):
-            nc.vector.quantize_mx(out=beams_codes[g][:].bitcast(FP8X4), scales=beams_plane[g][:],
-                                  in_=beams_i[g][:].rearrange("p b t -> p (b t)"))
-
-        def project(it, groups):
-            c, c0 = divmod(it * P, CH)
+        def project(tile_i, groups):
+            c, i0 = divmod(tile_i * P, CHUNK)
             if groups[0] == 0:
-                xbank["o", it] = ps_x.tile([P, 4, P], F32, name="xbank")
-            acc = xbank["o", it][:].rearrange("p t b -> p (t b)")
+                new_side_bank(("out", tile_i))
+            acc = side_bank["out", tile_i][:].rearrange("p t b -> p (t b)")
             for g in groups:
                 nc.tensor.matmul_mx(
                     out=acc,
-                    lhsT=cov_codes[g, c][:, c0:c0 + P].bitcast(FP8X4), lhsT_scale=cov_plane[g, c][:, c0:c0 + P],
+                    lhsT=cov_codes[g, c][:, i0:i0 + P].bitcast(FP8X4), lhsT_scale=cov_plane[g, c][:, i0:i0 + P],
                     rhs=beams_codes[g][:].bitcast(FP8X4), rhs_scale=beams_plane[g][:],
-                    start=(g == 0), stop=(g == G - 1))
+                    start=(g == 0), stop=(g == GROUPS - 1))
 
-        def store(it, on_vector=False):
-            res = work.tile([P, NB], F32, name="res", bufs=8)
-            acc = xbank["o", it][:].rearrange("p t b -> p (t b)")
+        def store(tile_i, on_vector=False):
+            res = work.tile([P, NB], F32, name="res", bufs=M // P)
+            acc = side_bank["out", tile_i][:].rearrange("p t b -> p (t b)")
+            gain = row_gain[:, tile_i:tile_i + 1]
             if on_vector:
-                nc.vector.tensor_scalar(out=res[:], in0=acc, scalar1=gains[:, 0, 16 + it:17 + it], scalar2=None, op0=ALU.mult)
+                nc.vector.tensor_scalar(out=res[:], in0=acc, scalar1=gain, scalar2=None, op0=ALU.mult)
             else:
-                nc.scalar.activation(out=res[:], in_=acc, func=ACT.Copy, scale=gains[:, 0, 16 + it:17 + it])
-            nc.sync.dma_start(out=out[P * it:P * (it + 1), :], in_=res[:])
+                nc.scalar.activation(out=res[:], in_=acc, func=ACT.Copy, scale=gain)
+            nc.sync.dma_start(out=out[P * tile_i:P * (tile_i + 1), :], in_=res[:])
 
-        def turn_gains():
-            bank = ps_x.tile([P, 4, P], F32, name="xbank")
-            for g in range(G):
-                nc.tensor.transpose(bank[:, g, :], d_rows32[:, P * g:P * (g + 1)], ident[:])
-            xbank["gains"] = bank
+        def steer_jobs(g):
+            return [("steer", g, half) for half in range(2)]
 
-        def copy_gains():
-            nc.scalar.copy(out=gains[:], in_=xbank["gains"][:, 0:G, 0:24])
+        def beams_jobs(g):
+            return [("beams", g, quarter) for quarter in range(4)]
 
-        def load_gains():
-            nc.sync.dma_start(out=d_rows[0:4, :].rearrange("t (q r) -> t q r", r=8),
-                              in_=d_col.rearrange("(q t r) -> t q r", t=4, r=8))
-            nc.sync.dma_start(out=d_rows[16:24, 0:P], in_=d_row.rearrange("(a p) -> a p", p=P))
+        jobs = (steer_jobs(0) + steer_jobs(1) + beams_jobs(0) + steer_jobs(2) + beams_jobs(1) + beams_jobs(2)
+                + [("out", tile_i) for tile_i in range(6)])
 
-        def taper_in():
-            nc.vector.tensor_copy(out=taper_i[:].rearrange("p (c i) t -> p c t i", i=4),
-                                  in_=taper_raw[:].rearrange("p t (c i) -> p c t i", i=4))
+        def jobs_of(r):
+            return jobs[2 * (r - 1):2 * r] if r >= 1 else []
 
-        def quantize_taper():
-            nc.vector.quantize_mx(out=taper_codes[:].bitcast(FP8X4), scales=taper_plane[:],
-                                  in_=taper_i[:].rearrange("p b t -> p (b t)"))
+        def on_vector(job):
+            return job in (("beams", 0, 1), ("beams", 1, 1))
+
+        def side_tensor(r):
+            for job in jobs_of(r):
+                if job[0] == "steer":
+                    turn_steer(job[1], job[2])
+                elif job[0] == "beams":
+                    beams(job[1], job[2])
+                else:
+                    project(job[1], list(range(GROUPS)))
+
+        def side_copies_vector(r):
+            for job in filter(on_vector, jobs_of(r)):
+                copy_beams(job[1], job[2], nc.vector.tensor_copy)
+
+        def side_copies_scalar(r):
+            for job in jobs_of(r):
+                if job[0] == "steer":
+                    copy_steer(job[1], job[2])
+                elif job[0] == "out":
+                    store(job[1])
+                elif not on_vector(job):
+                    copy_beams(job[1], job[2], nc.scalar.copy)
+
+        def side_quantize(r):
+            for job in jobs_of(r):
+                g = job[1]
+                if job == steer_jobs(g)[-1]:
+                    quantize(steer_codes[g][:], steer_plane[g][:], steer_t[g][:])
+                if job == beams_jobs(g)[-1]:
+                    quantize(beams_codes[g][:], beams_plane[g][:], beams_i[g][:].rearrange("p b t -> p (b t)"))
 
         nc.vector.memset(v_rawplane[0][:].bitcast(I32), 0)
         nc.vector.memset(u_plane[0][:].bitcast(I32), 0)
@@ -265,115 +287,64 @@ def tile_onebit_array_covariance_s12_kernel(
         load_codes(v_raw[0], vw, 0, 256)
         load_plane(v_rawplane[0], vs, 0, 128, range(1, 4))
         load_plane(u_plane[0], us, 0, 128)
-        loads = {
-            "u": lambda: load_codes(u_first[1], uw, 128, 256),
-            "d": load_gains,
-            "1": lambda: load_codes(v_raw[1], vw, 256, 512),
-            "p": lambda: load_plane(v_rawplane[1], vs, 128, 384),
-            "t": lambda: nc.sync.dma_start(out=taper_raw[:], in_=taper.rearrange("(p t) b -> p t b", t=4)),
-            "2": lambda: load_codes(v_raw[2], vw, 512, 768),
-            "a": lambda: load_steer(0), "b": lambda: load_steer(1), "c": lambda: load_steer(2),
-            "U": lambda: load_codes(u_late, uw, 256, 512),
-            "P": lambda: load_plane(u_plane[1], us, 128, 256),
-        }
-        for key in ORDER:
-            loads[key]()
-        nu = len(UNITS)
-        jobs = [("s", g, h) for g in range(G) for h in range(2)] + [("b", g, q) for g in range(G) for q in range(4)]
-        if BEAMS_EARLY:
-            jobs = jobs[0:4] + jobs[6:10] + jobs[4:6] + jobs[10:]
-        side = {}
-        at = {}
-        r = SIDE0
-        while jobs:
-            n = PER_S if jobs[0][0] == "s" else PER_B
-            side[r], jobs = jobs[:n], jobs[n:]
-            for j in side[r]:
-                at[j] = r
-            r = r + 1
-        vec = {}
-        for g in range(G):
-            vec.setdefault(at["s", g, 1] + QLAG, []).append(lambda g=g: quantize_steer(g))
-            vec.setdefault(at["b", g, 3] + QLAG, []).append(lambda g=g: quantize_beams(g))
-        r = max(at["b", G - 1, 3] + QLAG + 1, OUT0)
-        for c in range(3):
-            r = max(r, UNITS.index((G - 1, c)) + PLAG + 1)
-            side.setdefault(r, []).extend([("o", 2 * c), ("o", 2 * c + 1)])
-            r = r + 1
-        vec.setdefault(DEAL2, []).append(lambda: deal_v(2))
-
-        def side_tensor(r):
-            for item in side.get(r, []):
-                if item[0] == "s":
-                    turn_steer(item[1], item[2])
-                elif item[0] == "b":
-                    beams(item[1], item[2])
-                else:
-                    project(item[1], list(range(G)))
-
-        def side_copies(r, on_vector):
-            items = side.get(r, [])
-            for item in items:
-                if (r in VR and item == items[-1] and item[0] != "s") != on_vector:
-                    continue
-                if item[0] == "s":
-                    copy_steer(item[1], item[2], on_vector)
-                elif item[0] == "b":
-                    copy_beams(item[1], item[2], on_vector)
-                else:
-                    store(item[1], on_vector)
+        nc.sync.dma_start(out=taper_raw[:], in_=taper.rearrange("(p t) b -> p t b", t=4))
+        load_codes(u_first[1], uw, 128, 256)
+        load_gains()
+        load_codes(v_raw[1], vw, 256, 512)
+        load_plane(v_rawplane[1], vs, 128, 384)
+        load_plane(u_plane[1], us, 128, 256)
+        load_codes(v_raw[2], vw, 512, 768)
+        for g in range(GROUPS):
+            load_steer(g)
+        load_codes(u_late, uw, 256, 512)
 
         deal_v(0)
         for pair in range(2):
             gram(0, pair)
             to_turns(0, pair)
-        taper_in()
+        interleave_taper()
         nc.vector.tensor_copy(out=d_rows32[:], in_=d_rows[:])
-        quantize_taper()
+        quantize(taper_codes[:], taper_plane[:], taper_i[:].rearrange("p b t -> p (b t)"))
         deal_v(1)
-        for call in vec.get(-1, []):
-            call()
-        round_turns(0)
-        for r in range(1, AHEAD):
-            for pair in range(2):
-                gram(r, pair)
-                to_turns(r, pair)
-        last = nu - 1
-        for r in range(nu + PLAG - 1):
-            if r + AHEAD < nu:
-                gram(r + AHEAD, 0)
-                gram(r + AHEAD, 1)
+        new_whole(0)
+        round_turns(0, nc.vector, 0, COLS)
+
+        last = len(UNITS) - 1
+        for r in range(last + 1):
+            if r < last:
+                gram(r + 1, 0)
+                gram(r + 1, 1)
             if r == 0:
                 turn_gains()
             side_tensor(r)
-            if SINE_FIRST and 1 <= r <= last:
+            if r >= 1:
                 sine(r - 1)
-            if r + AHEAD < nu:
-                to_turns(r + AHEAD, 0)
-                to_turns(r + AHEAD, 1)
+            if r < last:
+                to_turns(r + 1, 0)
+                to_turns(r + 1, 1)
             if r == 0:
-                copy_gains()
-            if not SINE_FIRST and 1 <= r <= last:
-                sine(r - 1)
-            if r < nu:
-                reduce_turns(r)
-            if r >= PLAG:
-                scale_cov(r - PLAG)
-            side_copies(r, True)
-            if r + 1 < nu:
-                round_turns(r + 1)
-            if r >= PLAG:
-                quantize_cov(r - PLAG)
-            side_copies(r, False)
-            if r == last:
-                for half in range(2):
-                    sine(last, P * half, P * (half + 1))
-            for call in vec.get(r, []):
-                call()
-        for r in range(nu + PLAG - 1, nu + 4):
-            side_tensor(r)
-            side_copies(r, True)
-            side_copies(r, False)
+                nc.scalar.copy(out=row_gain[:], in_=gains[:, 0, GAIN_ROW:GAIN_ROW + M // P])
+            reduce_turns(r)
+            if r < last:
+                new_whole(r + 1)
+            if 1 <= r < last:
+                round_turns(r + 1, nc.gpsimd, 0, GPSIMD_COLS)
+            if r >= 1:
+                scale_cov(r - 1)
+            side_copies_vector(r)
+            if r < last:
+                round_turns(r + 1, nc.vector, GPSIMD_COLS if r >= 1 else 0, COLS)
+            if r >= 1:
+                quantize_cov(r - 1)
+            side_copies_scalar(r)
+            side_quantize(r)
+            if r == 0:
+                deal_v(2)
+
+        for half in range(2):
+            sine(last, P * half, P * (half + 1))
+        side_tensor(last + 1)
+        side_copies_scalar(last + 1)
         for half in range(2):
             project(6 + half, [0, 1])
         for half in range(2):

@@ -20,14 +20,18 @@ ALU = mybir.AluOpType
 P = 128
 PASSES = T // 512
 GROUPS = N // 512
+HALF = 512
 CHUNK = 256
-COLS = 4 * CHUNK
+COLS = 2 * HALF
+HALF_TILES = M // P // 2
 TURN = 2.0 * math.pi
 ROUND = 1.5 * 2.0 ** 23
-GPSIMD_COLS = 640
+GPSIMD_COLS = 512
 GAIN_ROW = 16
+FIRST_SIDE_ROUND = 2
 
-UNITS = [(g, c) for g in range(GROUPS) for c in (0, 1)] + [(g, c) for c in (2, 3) for g in range(GROUPS)]
+BLOCKS = [(g, h) for h in range(2) for g in range(GROUPS)]
+STEPS = 2 * len(BLOCKS)
 
 
 def tile_onebit_array_covariance_s12_kernel(
@@ -47,9 +51,8 @@ def tile_onebit_array_covariance_s12_kernel(
         uw, vw = u_words.bitcast(I32), v_words.bitcast(I32)
         us, vs = u_scales.bitcast(I32), v_scales.bitcast(I32)
 
-        u_first = [kept("u_codes%d" % c, [P, PASSES, 2 * CHUNK], U8) for c in range(2)]
-        u_late = kept("u_late", [P, PASSES, 4 * CHUNK], U8)
-        u_plane = [kept("u_plane%d" % h, [P, PASSES, 2 * CHUNK], U8) for h in range(2)]
+        u_codes = [kept("u_codes%d" % h, [P, PASSES, 2 * HALF], U8) for h in range(2)]
+        u_plane = [kept("u_plane%d" % h, [P, PASSES, HALF], U8) for h in range(2)]
         v_raw = [kept("v_raw%d" % g, [P, PASSES, 1024], U8) for g in range(GROUPS)]
         v_rawplane = [kept("v_rawplane0", [P, PASSES, 512], U8),
                       kept("v_rawplane1", [P, PASSES, 1024], U8)]
@@ -66,12 +69,11 @@ def tile_onebit_array_covariance_s12_kernel(
         beams_i = [kept("beams_i%d" % g, [P, NB, 4], BF16) for g in range(GROUPS)]
         beams_codes = [kept("beams_codes%d" % g, [P, NB], U32) for g in range(GROUPS)]
         beams_plane = [kept("beams_plane%d" % g, [P, NB], U8) for g in range(GROUPS)]
-        cov_codes = {unit: kept("cov_codes%d_%d" % unit, [P, CHUNK], U32) for unit in UNITS}
-        cov_plane = {unit: kept("cov_plane%d_%d" % unit, [P, CHUNK], U8) for unit in UNITS}
+        cov_codes = [kept("cov_codes%d" % r, [P, CHUNK], U32) for r in range(STEPS)]
+        cov_plane = [kept("cov_plane%d" % r, [P, CHUNK], U8) for r in range(STEPS)]
         d_rows = kept("d_rows", [P, GROUPS * P], BF16)
         d_rows32 = kept("d_rows32", [P, GROUPS * P], F32)
         ident = kept("ident", [P, P], F32)
-        warm = kept("warm", [P, 2], F32)
         gains = gain_bank.tile([P, GROUPS, P], F32, name="gains")
         row_gain = kept("row_gain", [P, M // P], F32)
 
@@ -117,60 +119,56 @@ def tile_onebit_array_covariance_s12_kernel(
 
         banks, turns, whole, frac, sines, cov = {}, {}, {}, {}, {}, {}
 
-        def gram(r, pair):
-            g, c = UNITS[r]
-            h, i0 = divmod(c * CHUNK, 2 * CHUNK)
-            bank = gram_banks.tile([P, 2, CHUNK], F32, name="gram")
-            banks[r, pair] = bank
-            for e in range(2):
-                t = 2 * pair + e
-                for k in range(PASSES):
-                    rows = u_late[:, k, 2 * i0:2 * (i0 + CHUNK)] if h else u_first[c][:, k, :]
-                    nc.tensor.matmul_mx(
-                        out=bank[:, e, :],
-                        lhsT=v_codes[g][:, k, t, :].bitcast(FP4X4), lhsT_scale=v_plane[g][:, k, t, :],
-                        rhs=rows.bitcast(FP4X4), rhs_scale=u_plane[h][:, k, i0:i0 + CHUNK],
-                        start=(k == 0), stop=(k == PASSES - 1))
+        def gram(r, e):
+            g, h = BLOCKS[r // 2]
+            t = 2 * (r % 2) + e
+            banks[r, e] = gram_banks.tile([P, HALF], F32, name="gram")
+            for k in range(PASSES):
+                nc.tensor.matmul_mx(
+                    out=banks[r, e][:],
+                    lhsT=v_codes[g][:, k, t, :].bitcast(FP4X4), lhsT_scale=v_plane[g][:, k, t, :],
+                    rhs=u_codes[h][:, k, :].bitcast(FP4X4), rhs_scale=u_plane[h][:, k, :],
+                    start=(k == 0), stop=(k == PASSES - 1))
 
-        def to_turns(r, pair):
-            if pair == 0:
-                turns[r] = work.tile([P, 2, CHUNK, 2], F32, name="turns")
-            nc.scalar.activation(out=turns[r][:, pair, :, :], in_=banks[r, pair][:].rearrange("p e i -> p i e"),
+        def to_turns(r, e):
+            if e == 0:
+                turns[r] = work.tile([P, COLS], F32, name="turns", bufs=4)
+            nc.scalar.activation(out=turns[r][:, HALF * e:HALF * (e + 1)], in_=banks[r, e][:],
                                  func=ACT.Copy, scale=1.0 / TURN)
 
         def new_whole(r):
             whole[r] = work.tile([P, COLS], I32, name="whole", bufs=1)
 
         def round_turns(r, engine, c0, c1):
-            engine.tensor_scalar(out=whole[r][:, c0:c1],
-                                 in0=turns[r][:].rearrange("p a i e -> p (a i e)")[:, c0:c1],
+            engine.tensor_scalar(out=whole[r][:, c0:c1], in0=turns[r][:, c0:c1],
                                  scalar1=1.0, scalar2=ROUND, op0=ALU.mult, op1=ALU.add)
 
-        def reduce_turns(r):
-            frac[r] = work.tile([P, COLS], F32, name="frac")
-            nc.vector.scalar_tensor_tensor(out=frac[r][:], in0=whole[r][:], scalar=ROUND,
-                                           in1=turns[r][:].rearrange("p a i e -> p (a i e)"),
-                                           op0=ALU.subtract, op1=ALU.subtract)
+        def reduce_turns(r, c0=0, c1=COLS):
+            if c0 == 0:
+                frac[r] = work.tile([P, COLS], F32, name="frac")
+            nc.vector.scalar_tensor_tensor(out=frac[r][:, c0:c1], in0=whole[r][:, c0:c1], scalar=ROUND,
+                                           in1=turns[r][:, c0:c1], op0=ALU.subtract, op1=ALU.subtract)
 
-        def sine(r, i0=0, i1=CHUNK):
-            if i0 == 0:
-                sines[r] = work.tile([P, 2, CHUNK, 2], F32, name="sines", bufs=4)
-            nc.scalar.activation(out=sines[r][:, :, i0:i1, :],
-                                 in_=frac[r][:].rearrange("p (a i e) -> p a i e", a=2, e=2)[:, :, i0:i1, :],
+        def sine(r, i0=0, i1=HALF, e0=0, e1=2):
+            if r % 2 == 0 and e0 == 0:
+                sines[r // 2] = work.tile([P, 4, HALF], F32, name="sines")
+            t0 = 2 * (r % 2)
+            nc.scalar.activation(out=sines[r // 2][:, t0 + e0:t0 + e1, i0:i1],
+                                 in_=frac[r][:].rearrange("p (e i) -> p e i", e=2)[:, e0:e1, i0:i1],
                                  func=ACT.Sin, scale=-TURN)
 
         def scale_cov(r, i0=0, i1=CHUNK):
-            g = UNITS[r][0]
+            g = BLOCKS[r // 2][0]
             if i0 == 0:
-                cov[r] = work.tile([P, CHUNK, 2, 2], BF16, name="cov", align_bytes=64)
-            gain = gains[:, g, 0:4].rearrange("p (o a e) -> p o a e", o=1, a=2)
-            nc.vector.tensor_tensor(out=cov[r][:, i0:i1],
-                                    in0=sines[r][:, :, i0:i1, :].rearrange("p a i e -> p i a e"),
-                                    in1=gain.to_broadcast([P, i1 - i0, 2, 2]), op=ALU.mult)
+                cov[r] = work.tile([P, CHUNK, 4], BF16, name="cov", align_bytes=64)
+            rows = slice((r % 2) * CHUNK + i0, (r % 2) * CHUNK + i1)
+            gain = gains[:, g, 0:4].rearrange("p (c t i) -> p c t i", c=1, i=1)
+            nc.vector.tensor_tensor(out=cov[r][:, i0:i1].rearrange("p (c i) t -> p c t i", i=2),
+                                    in0=sines[r // 2][:, :, rows].rearrange("p t (c i) -> p c t i", i=2),
+                                    in1=gain.to_broadcast([P, (i1 - i0) // 2, 4, 2]), op=ALU.mult)
 
         def quantize_cov(r, i0=0, i1=CHUNK):
-            quantize(cov_codes[UNITS[r]][:, i0:i1], cov_plane[UNITS[r]][:, i0:i1],
-                     cov[r][:, i0:i1].rearrange("p i a e -> p (i a e)"))
+            quantize(cov_codes[r][:, i0:i1], cov_plane[r][:, i0:i1], cov[r][:, i0:i1].rearrange("p i t -> p (i t)"))
 
 
         side_bank = {}
@@ -207,20 +205,23 @@ def tile_onebit_array_covariance_s12_kernel(
                  in_=side_bank["beams", g, quarter][:].rearrange("p t b -> p b t"))
 
         def project(tile_i, groups):
-            c, i0 = divmod(tile_i * P, CHUNK)
+            h, row0 = divmod(tile_i * P, HALF)
+            c, i0 = divmod(row0, CHUNK)
             if groups[0] == 0:
-                new_side_bank(("out", tile_i))
-            acc = side_bank["out", tile_i][:].rearrange("p t b -> p (t b)")
+                pool, name = (gram_banks, "gram") if tile_i >= HALF_TILES else (side_banks, "side_bank")
+                side_bank["out", tile_i] = pool.tile([P, NB], F32, name=name)
+            acc = side_bank["out", tile_i][:]
             for g in groups:
+                r = 2 * BLOCKS.index((g, h)) + c
                 nc.tensor.matmul_mx(
                     out=acc,
-                    lhsT=cov_codes[g, c][:, i0:i0 + P].bitcast(FP8X4), lhsT_scale=cov_plane[g, c][:, i0:i0 + P],
+                    lhsT=cov_codes[r][:, i0:i0 + P].bitcast(FP8X4), lhsT_scale=cov_plane[r][:, i0:i0 + P],
                     rhs=beams_codes[g][:].bitcast(FP8X4), rhs_scale=beams_plane[g][:],
                     start=(g == 0), stop=(g == GROUPS - 1))
 
         def store(tile_i, on_vector=False):
             res = work.tile([P, NB], F32, name="res", bufs=M // P)
-            acc = side_bank["out", tile_i][:].rearrange("p t b -> p (t b)")
+            acc = side_bank["out", tile_i][:]
             gain = row_gain[:, tile_i:tile_i + 1]
             if on_vector:
                 nc.vector.tensor_scalar(out=res[:], in0=acc, scalar1=gain, scalar2=None, op0=ALU.mult)
@@ -235,13 +236,17 @@ def tile_onebit_array_covariance_s12_kernel(
             return [("beams", g, quarter) for quarter in range(4)]
 
         jobs = (steer_jobs(0) + steer_jobs(1) + beams_jobs(0) + steer_jobs(2) + beams_jobs(1) + beams_jobs(2)
-                + [("out", tile_i) for tile_i in range(6)])
+                + [("out", tile_i) for tile_i in range(HALF_TILES)])
+
+        def jobs_before(r):
+            rounds = max(r - FIRST_SIDE_ROUND, 0)
+            return 2 * rounds + min(max(rounds - 1, 0), 2)
 
         def jobs_of(r):
-            return jobs[2 * (r - 1):2 * r] if r >= 1 else []
+            return jobs[jobs_before(r):jobs_before(r + 1)]
 
-        def on_vector(job):
-            return job in (("beams", 0, 1), ("beams", 1, 1))
+        def vector_empties(job):
+            return job[0] == "beams" and job[1] < 2 and job[2] == 1
 
         def side_tensor(r):
             for job in jobs_of(r):
@@ -253,7 +258,7 @@ def tile_onebit_array_covariance_s12_kernel(
                     project(job[1], list(range(GROUPS)))
 
         def side_copies_vector(r):
-            for job in filter(on_vector, jobs_of(r)):
+            for job in filter(vector_empties, jobs_of(r)):
                 copy_beams(job[1], job[2], nc.vector.tensor_copy)
 
         def side_copies_scalar(r):
@@ -262,7 +267,7 @@ def tile_onebit_array_covariance_s12_kernel(
                     copy_steer(job[1], job[2])
                 elif job[0] == "out":
                     store(job[1])
-                elif not on_vector(job):
+                elif not vector_empties(job):
                     copy_beams(job[1], job[2], nc.scalar.copy)
 
         def side_quantize(r):
@@ -275,20 +280,17 @@ def tile_onebit_array_covariance_s12_kernel(
 
         nc.vector.memset(v_rawplane[0][:].bitcast(I32), 0)
         nc.vector.memset(u_plane[0][:].bitcast(I32), 0)
-        nc.vector.memset(warm[:, 0:1], 0.0)
-        nc.scalar.activation(out=warm[:, 1:2], in_=warm[:, 0:1], func=ACT.Sin)
         nc.vector.memset(d_rows[:], 0.0)
         nc.vector.memset(v_rawplane[1][:].bitcast(I32), 0)
         nc.vector.memset(u_plane[1][:].bitcast(I32), 0)
         make_identity(nc, ident[:])
 
-        load_codes(u_first[0], uw, 0, 128)
-        load_plane(v_rawplane[0], vs, 0, 128, range(1))
         load_codes(v_raw[0], vw, 0, 256)
+        load_plane(v_rawplane[0], vs, 0, 128, range(1))
+        load_codes(u_codes[0], uw, 0, 256)
         load_plane(v_rawplane[0], vs, 0, 128, range(1, 4))
         load_plane(u_plane[0], us, 0, 128)
         nc.sync.dma_start(out=taper_raw[:], in_=taper.rearrange("(p t) b -> p t b", t=4))
-        load_codes(u_first[1], uw, 128, 256)
         load_gains()
         load_codes(v_raw[1], vw, 256, 512)
         load_plane(v_rawplane[1], vs, 128, 384)
@@ -296,61 +298,70 @@ def tile_onebit_array_covariance_s12_kernel(
         load_codes(v_raw[2], vw, 512, 768)
         for g in range(GROUPS):
             load_steer(g)
-        load_codes(u_late, uw, 256, 512)
+        load_codes(u_codes[1], uw, 256, 512)
 
         deal_v(0)
-        for pair in range(2):
-            gram(0, pair)
-            to_turns(0, pair)
+        gram(0, 0)
+        gram(0, 1)
+        to_turns(0, 0)
+        new_whole(0)
         interleave_taper()
+        round_turns(0, nc.vector, 0, HALF)
         nc.vector.tensor_copy(out=d_rows32[:], in_=d_rows[:])
+        reduce_turns(0, 0, HALF)
+        sine(0, e1=1)
+        to_turns(0, 1)
         quantize(taper_codes[:], taper_plane[:], taper_i[:].rearrange("p b t -> p (b t)"))
         deal_v(1)
-        new_whole(0)
-        round_turns(0, nc.vector, 0, COLS)
+        round_turns(0, nc.vector, HALF, COLS)
 
-        last = len(UNITS) - 1
-        for r in range(last + 1):
+        last = STEPS - 1
+        for r in range(STEPS):
+            scales = r >= 2
             if r < last:
                 gram(r + 1, 0)
                 gram(r + 1, 1)
-            if r == 0:
+            if r == FIRST_SIDE_ROUND:
                 turn_gains()
             side_tensor(r)
             if r >= 1:
-                sine(r - 1)
+                sine(r - 1, e0=1 if r == 1 else 0)
             if r < last:
                 to_turns(r + 1, 0)
                 to_turns(r + 1, 1)
-            if r == 0:
-                nc.scalar.copy(out=row_gain[:], in_=gains[:, 0, GAIN_ROW:GAIN_ROW + M // P])
-            reduce_turns(r)
+            reduce_turns(r, HALF if r == 0 else 0)
             if r < last:
                 new_whole(r + 1)
-            if 1 <= r < last:
+            if scales and r < last:
                 round_turns(r + 1, nc.gpsimd, 0, GPSIMD_COLS)
-            if r >= 1:
-                scale_cov(r - 1)
+            if scales:
+                scale_cov(r - 2)
             side_copies_vector(r)
             if r < last:
-                round_turns(r + 1, nc.vector, GPSIMD_COLS if r >= 1 else 0, COLS)
-            if r >= 1:
-                quantize_cov(r - 1)
+                round_turns(r + 1, nc.vector, GPSIMD_COLS if scales else 0, COLS)
+            if scales:
+                quantize_cov(r - 2)
+            if r == last:
+                for c in range(2):
+                    sine(last, CHUNK * c, CHUNK * (c + 1))
             side_copies_scalar(r)
+            if r == FIRST_SIDE_ROUND + 1:
+                nc.scalar.copy(out=row_gain[:], in_=gains[:, 0, GAIN_ROW:GAIN_ROW + M // P])
             side_quantize(r)
             if r == 0:
                 deal_v(2)
 
-        for half in range(2):
-            sine(last, P * half, P * (half + 1))
-        side_tensor(last + 1)
-        side_copies_scalar(last + 1)
-        for half in range(2):
-            project(6 + half, [0, 1])
-        for half in range(2):
-            scale_cov(last, P * half, P * (half + 1))
-        for half in range(2):
-            quantize_cov(last, P * half, P * (half + 1))
-            project(6 + half, [2])
-        store(6)
-        store(7, on_vector=True)
+        for tile_i in range(HALF_TILES, 2 * HALF_TILES):
+            project(tile_i, [0, 1])
+        scale_cov(last - 1)
+        quantize_cov(last - 1)
+        scale_cov(last, 0, P)
+        for part in range(2):
+            project(HALF_TILES + part, [2])
+            store(HALF_TILES + part)
+        scale_cov(last, P, 2 * P)
+        for part in range(2):
+            quantize_cov(last, P * part, P * (part + 1))
+            project(HALF_TILES + 2 + part, [2])
+        store(HALF_TILES + 2)
+        store(HALF_TILES + 3, on_vector=True)

import math
from contextlib import ExitStack

import concourse.mybir as mybir
from concourse.masks import make_identity

M, T, N, L, NB = 1024, 2048, 1536, 512, 512
FLOPS = 2 * M * N * T + 2 * N * L * NB + 2 * M * N * NB

F32 = mybir.dt.float32
BF16 = mybir.dt.bfloat16
I32 = mybir.dt.int32
U32 = mybir.dt.uint32
U8 = mybir.dt.uint8
FP8X4 = mybir.dt.float8_e4m3fn_x4
FP4X4 = mybir.dt.float4_e2m1fn_x4
ACT = mybir.ActivationFunctionType
ALU = mybir.AluOpType

P = 128
PASSES = T // 512
GROUPS = N // 512
HALF = 512
CHUNK = 256
COLS = 2 * HALF
HALF_TILES = M // P // 2
TURN = 2.0 * math.pi
ROUND = 1.5 * 2.0 ** 23
GPSIMD_COLS = 512
GAIN_ROW = 16
FIRST_SIDE_ROUND = 2

BLOCKS = [(g, h) for h in range(2) for g in range(GROUPS)]
STEPS = 2 * len(BLOCKS)


def tile_onebit_array_covariance_s12_kernel(
        tc, u_words, u_scales, v_words, v_scales, d_row, d_col, steer, taper, out):
    nc = tc.nc
    with ExitStack() as ctx:
        keep = ctx.enter_context(tc.tile_pool(name="keep", bufs=1))
        work = ctx.enter_context(tc.tile_pool(name="work", bufs=3))
        gram_banks = ctx.enter_context(tc.psum_pool(name="gram_banks", bufs=4))
        side_banks = ctx.enter_context(tc.psum_pool(name="side_banks", bufs=3))
        gain_bank = ctx.enter_context(tc.psum_pool(name="gain_bank", bufs=1))
        ctx.enter_context(tc.manual_schedule())

        def kept(name, shape, dtype):
            return keep.tile(shape, dtype, name=name, align_bytes=64)

        uw, vw = u_words.bitcast(I32), v_words.bitcast(I32)
        us, vs = u_scales.bitcast(I32), v_scales.bitcast(I32)

        u_codes = [kept("u_codes%d" % h, [P, PASSES, 2 * HALF], U8) for h in range(2)]
        u_plane = [kept("u_plane%d" % h, [P, PASSES, HALF], U8) for h in range(2)]
        v_raw = [kept("v_raw%d" % g, [P, PASSES, 1024], U8) for g in range(GROUPS)]
        v_rawplane = [kept("v_rawplane0", [P, PASSES, 512], U8),
                      kept("v_rawplane1", [P, PASSES, 1024], U8)]
        v_codes = [kept("v_codes%d" % g, [P, PASSES, 4, 2 * P], U8) for g in range(GROUPS)]
        v_plane = [kept("v_plane%d" % g, [P, PASSES, 4, P], U8) for g in range(GROUPS)]
        steer_raw = [kept("steer_raw%d" % g, [P, 4 * L], BF16) for g in range(GROUPS)]
        steer_t = [kept("steer_t%d" % g, [P, 4 * 512], BF16) for g in range(GROUPS)]
        steer_codes = [kept("steer_codes%d" % g, [P, 512], U32) for g in range(GROUPS)]
        steer_plane = [kept("steer_plane%d" % g, [P, 512], U8) for g in range(GROUPS)]
        taper_raw = kept("taper_raw", [P, 4, NB], BF16)
        taper_i = kept("taper_i", [P, NB, 4], BF16)
        taper_codes = kept("taper_codes", [P, NB], U32)
        taper_plane = kept("taper_plane", [P, NB], U8)
        beams_i = [kept("beams_i%d" % g, [P, NB, 4], BF16) for g in range(GROUPS)]
        beams_codes = [kept("beams_codes%d" % g, [P, NB], U32) for g in range(GROUPS)]
        beams_plane = [kept("beams_plane%d" % g, [P, NB], U8) for g in range(GROUPS)]
        cov_codes = [kept("cov_codes%d" % r, [P, CHUNK], U32) for r in range(STEPS)]
        cov_plane = [kept("cov_plane%d" % r, [P, CHUNK], U8) for r in range(STEPS)]
        d_rows = kept("d_rows", [P, GROUPS * P], BF16)
        d_rows32 = kept("d_rows32", [P, GROUPS * P], F32)
        ident = kept("ident", [P, P], F32)
        gains = gain_bank.tile([P, GROUPS, P], F32, name="gains")
        row_gain = kept("row_gain", [P, M // P], F32)


        def load_codes(dst, src, w0, w1):
            nc.sync.dma_start(out=dst[:].bitcast(I32), in_=src[:, :, w0:w1].rearrange("k p w -> p k w"))

        def load_plane(dst, src, w0, w1, quadrants=range(4)):
            for q in quadrants:
                nc.sync.dma_start(out=dst[32 * q:32 * q + 4, :, :].bitcast(I32),
                                  in_=src[:, 4 * q:4 * q + 4, w0:w1].rearrange("k r w -> r k w"))

        def load_steer(g):
            nc.sync.dma_start(out=steer_raw[g][:],
                              in_=steer[512 * g:512 * (g + 1), :].rearrange("(s a) l -> s (a l)", a=4))

        def load_gains():
            nc.sync.dma_start(out=d_rows[0:4, :].rearrange("t (q r) -> t q r", r=8),
                              in_=d_col.rearrange("(q t r) -> t q r", t=4, r=8))
            nc.sync.dma_start(out=d_rows[GAIN_ROW:GAIN_ROW + M // P, 0:P], in_=d_row.rearrange("(a p) -> a p", p=P))


        def deal_v(g):
            nc.vector.tensor_copy(
                out=v_codes[g][:].bitcast(I32).rearrange("p k t (q w) -> p k t q w", w=4),
                in_=v_raw[g][:].bitcast(I32).rearrange("p k (q t w) -> p k t q w", t=4, w=4))
            raw = v_rawplane[0][:] if g == 0 else v_rawplane[1][:, :, 512 * (g - 1):512 * g]
            nc.vector.tensor_copy(
                out=v_plane[g][:].bitcast(I32).rearrange("p k t (q w) -> p k t q w", w=2),
                in_=raw.bitcast(I32).rearrange("p k (q t w) -> p k t q w", t=4, w=2))

        def interleave_taper():
            nc.vector.tensor_copy(out=taper_i[:].rearrange("p (c i) t -> p c t i", i=4),
                                  in_=taper_raw[:].rearrange("p t (c i) -> p c t i", i=4))

        def quantize(codes, plane, values):
            nc.vector.quantize_mx(out=codes.bitcast(FP8X4), scales=plane, in_=values)

        def turn_gains():
            for g in range(GROUPS):
                nc.tensor.transpose(gains[:, g, :], d_rows32[:, P * g:P * (g + 1)], ident[:])


        banks, turns, whole, frac, sines, cov = {}, {}, {}, {}, {}, {}

        def gram(r, e):
            g, h = BLOCKS[r // 2]
            t = 2 * (r % 2) + e
            banks[r, e] = gram_banks.tile([P, HALF], F32, name="gram")
            for k in range(PASSES):
                nc.tensor.matmul_mx(
                    out=banks[r, e][:],
                    lhsT=v_codes[g][:, k, t, :].bitcast(FP4X4), lhsT_scale=v_plane[g][:, k, t, :],
                    rhs=u_codes[h][:, k, :].bitcast(FP4X4), rhs_scale=u_plane[h][:, k, :],
                    start=(k == 0), stop=(k == PASSES - 1))

        def to_turns(r, e):
            if e == 0:
                turns[r] = work.tile([P, COLS], F32, name="turns", bufs=4)
            nc.scalar.activation(out=turns[r][:, HALF * e:HALF * (e + 1)], in_=banks[r, e][:],
                                 func=ACT.Copy, scale=1.0 / TURN)

        def new_whole(r):
            whole[r] = work.tile([P, COLS], I32, name="whole", bufs=1)

        def round_turns(r, engine, c0, c1):
            engine.tensor_scalar(out=whole[r][:, c0:c1], in0=turns[r][:, c0:c1],
                                 scalar1=1.0, scalar2=ROUND, op0=ALU.mult, op1=ALU.add)

        def reduce_turns(r, c0=0, c1=COLS):
            if c0 == 0:
                frac[r] = work.tile([P, COLS], F32, name="frac")
            nc.vector.scalar_tensor_tensor(out=frac[r][:, c0:c1], in0=whole[r][:, c0:c1], scalar=ROUND,
                                           in1=turns[r][:, c0:c1], op0=ALU.subtract, op1=ALU.subtract)

        def sine(r, i0=0, i1=HALF, e0=0, e1=2):
            if r % 2 == 0 and e0 == 0:
                sines[r // 2] = work.tile([P, 4, HALF], F32, name="sines")
            t0 = 2 * (r % 2)
            nc.scalar.activation(out=sines[r // 2][:, t0 + e0:t0 + e1, i0:i1],
                                 in_=frac[r][:].rearrange("p (e i) -> p e i", e=2)[:, e0:e1, i0:i1],
                                 func=ACT.Sin, scale=-TURN)

        def scale_cov(r, i0=0, i1=CHUNK):
            g = BLOCKS[r // 2][0]
            if i0 == 0:
                cov[r] = work.tile([P, CHUNK, 4], BF16, name="cov", align_bytes=64)
            rows = slice((r % 2) * CHUNK + i0, (r % 2) * CHUNK + i1)
            gain = gains[:, g, 0:4].rearrange("p (c t i) -> p c t i", c=1, i=1)
            nc.vector.tensor_tensor(out=cov[r][:, i0:i1].rearrange("p (c i) t -> p c t i", i=2),
                                    in0=sines[r // 2][:, :, rows].rearrange("p t (c i) -> p c t i", i=2),
                                    in1=gain.to_broadcast([P, (i1 - i0) // 2, 4, 2]), op=ALU.mult)

        def quantize_cov(r, i0=0, i1=CHUNK):
            quantize(cov_codes[r][:, i0:i1], cov_plane[r][:, i0:i1], cov[r][:, i0:i1].rearrange("p i t -> p (i t)"))


        side_bank = {}

        def new_side_bank(job):
            side_bank[job] = side_banks.tile([P, 4, P], F32, name="side_bank")
            return side_bank[job]

        def turn_steer(g, half):
            bank = new_side_bank(("steer", g, half))
            words = steer_raw[g][:].bitcast(F32)
            for x in range(4):
                a, u = 2 * half + x // 2, x % 2
                nc.tensor.transpose(bank[:, x, :], words[:, 256 * a + u:256 * (a + 1):2], ident[:])

        def copy_steer(g, half):
            dst = steer_t[g][:].bitcast(F32).rearrange("p (t q h f x) -> p f q t h x", t=4, q=16, h=2, f=2)
            nc.scalar.copy(out=dst[:, half],
                           in_=side_bank["steer", g, half][:].rearrange("p x (q t h) -> p q t h x", t=4, h=2))

        def beams(g, quarter):
            bank = new_side_bank(("beams", g, quarter))
            cols = slice(P * quarter, P * (quarter + 1))
            for t in range(4):
                nc.tensor.matmul_mx(
                    out=bank[:, t, :],
                    lhsT=steer_codes[g][:, P * t:P * (t + 1)].bitcast(FP8X4),
                    lhsT_scale=steer_plane[g][:, P * t:P * (t + 1)],
                    rhs=taper_codes[:, cols].bitcast(FP8X4), rhs_scale=taper_plane[:, cols],
                    start=True, stop=True)

        def copy_beams(g, quarter, copy):
            copy(out=beams_i[g][:, P * quarter:P * (quarter + 1), :],
                 in_=side_bank["beams", g, quarter][:].rearrange("p t b -> p b t"))

        def project(tile_i, groups):
            h, row0 = divmod(tile_i * P, HALF)
            c, i0 = divmod(row0, CHUNK)
            if groups[0] == 0:
                pool, name = (gram_banks, "gram") if tile_i >= HALF_TILES else (side_banks, "side_bank")
                side_bank["out", tile_i] = pool.tile([P, NB], F32, name=name)
            acc = side_bank["out", tile_i][:]
            for g in groups:
                r = 2 * BLOCKS.index((g, h)) + c
                nc.tensor.matmul_mx(
                    out=acc,
                    lhsT=cov_codes[r][:, i0:i0 + P].bitcast(FP8X4), lhsT_scale=cov_plane[r][:, i0:i0 + P],
                    rhs=beams_codes[g][:].bitcast(FP8X4), rhs_scale=beams_plane[g][:],
                    start=(g == 0), stop=(g == GROUPS - 1))

        def store(tile_i, on_vector=False):
            res = work.tile([P, NB], F32, name="res", bufs=M // P)
            acc = side_bank["out", tile_i][:]
            gain = row_gain[:, tile_i:tile_i + 1]
            if on_vector:
                nc.vector.tensor_scalar(out=res[:], in0=acc, scalar1=gain, scalar2=None, op0=ALU.mult)
            else:
                nc.scalar.activation(out=res[:], in_=acc, func=ACT.Copy, scale=gain)
            nc.sync.dma_start(out=out[P * tile_i:P * (tile_i + 1), :], in_=res[:])

        def steer_jobs(g):
            return [("steer", g, half) for half in range(2)]

        def beams_jobs(g):
            return [("beams", g, quarter) for quarter in range(4)]

        jobs = (steer_jobs(0) + steer_jobs(1) + beams_jobs(0) + steer_jobs(2) + beams_jobs(1) + beams_jobs(2)
                + [("out", tile_i) for tile_i in range(HALF_TILES)])

        def jobs_before(r):
            rounds = max(r - FIRST_SIDE_ROUND, 0)
            return 2 * rounds + min(max(rounds - 1, 0), 2)

        def jobs_of(r):
            return jobs[jobs_before(r):jobs_before(r + 1)]

        def vector_empties(job):
            return job[0] == "beams" and job[1] < 2 and job[2] == 1

        def side_tensor(r):
            for job in jobs_of(r):
                if job[0] == "steer":
                    turn_steer(job[1], job[2])
                elif job[0] == "beams":
                    beams(job[1], job[2])
                else:
                    project(job[1], list(range(GROUPS)))

        def side_copies_vector(r):
            for job in filter(vector_empties, jobs_of(r)):
                copy_beams(job[1], job[2], nc.vector.tensor_copy)

        def side_copies_scalar(r):
            for job in jobs_of(r):
                if job[0] == "steer":
                    copy_steer(job[1], job[2])
                elif job[0] == "out":
                    store(job[1])
                elif not vector_empties(job):
                    copy_beams(job[1], job[2], nc.scalar.copy)

        def side_quantize(r):
            for job in jobs_of(r):
                g = job[1]
                if job == steer_jobs(g)[-1]:
                    quantize(steer_codes[g][:], steer_plane[g][:], steer_t[g][:])
                if job == beams_jobs(g)[-1]:
                    quantize(beams_codes[g][:], beams_plane[g][:], beams_i[g][:].rearrange("p b t -> p (b t)"))

        nc.vector.memset(v_rawplane[0][:].bitcast(I32), 0)
        nc.vector.memset(u_plane[0][:].bitcast(I32), 0)
        nc.vector.memset(d_rows[:], 0.0)
        nc.vector.memset(v_rawplane[1][:].bitcast(I32), 0)
        nc.vector.memset(u_plane[1][:].bitcast(I32), 0)
        make_identity(nc, ident[:])

        load_codes(v_raw[0], vw, 0, 256)
        load_plane(v_rawplane[0], vs, 0, 128, range(1))
        load_codes(u_codes[0], uw, 0, 256)
        load_plane(v_rawplane[0], vs, 0, 128, range(1, 4))
        load_plane(u_plane[0], us, 0, 128)
        nc.sync.dma_start(out=taper_raw[:], in_=taper.rearrange("(p t) b -> p t b", t=4))
        load_gains()
        load_codes(v_raw[1], vw, 256, 512)
        load_plane(v_rawplane[1], vs, 128, 384)
        load_plane(u_plane[1], us, 128, 256)
        load_codes(v_raw[2], vw, 512, 768)
        for g in range(GROUPS):
            load_steer(g)
        load_codes(u_codes[1], uw, 256, 512)

        deal_v(0)
        gram(0, 0)
        gram(0, 1)
        to_turns(0, 0)
        new_whole(0)
        interleave_taper()
        round_turns(0, nc.vector, 0, HALF)
        nc.vector.tensor_copy(out=d_rows32[:], in_=d_rows[:])
        reduce_turns(0, 0, HALF)
        sine(0, e1=1)
        to_turns(0, 1)
        quantize(taper_codes[:], taper_plane[:], taper_i[:].rearrange("p b t -> p (b t)"))
        deal_v(1)
        round_turns(0, nc.vector, HALF, COLS)

        last = STEPS - 1
        for r in range(STEPS):
            scales = r >= 2
            if r < last:
                gram(r + 1, 0)
                gram(r + 1, 1)
            if r == FIRST_SIDE_ROUND:
                turn_gains()
            side_tensor(r)
            if r >= 1:
                sine(r - 1, e0=1 if r == 1 else 0)
            if r < last:
                to_turns(r + 1, 0)
                to_turns(r + 1, 1)
            reduce_turns(r, HALF if r == 0 else 0)
            if r < last:
                new_whole(r + 1)
            if scales and r < last:
                round_turns(r + 1, nc.gpsimd, 0, GPSIMD_COLS)
            if scales:
                scale_cov(r - 2)
            side_copies_vector(r)
            if r < last:
                round_turns(r + 1, nc.vector, GPSIMD_COLS if scales else 0, COLS)
            if scales:
                quantize_cov(r - 2)
            if r == last:
                for c in range(2):
                    sine(last, CHUNK * c, CHUNK * (c + 1))
            side_copies_scalar(r)
            if r == FIRST_SIDE_ROUND + 1:
                nc.scalar.copy(out=row_gain[:], in_=gains[:, 0, GAIN_ROW:GAIN_ROW + M // P])
            side_quantize(r)
            if r == 0:
                deal_v(2)

        for tile_i in range(HALF_TILES, 2 * HALF_TILES):
            project(tile_i, [0, 1])
        scale_cov(last - 1)
        quantize_cov(last - 1)
        scale_cov(last, 0, P)
        for part in range(2):
            project(HALF_TILES + part, [2])
            store(HALF_TILES + part)
        scale_cov(last, P, 2 * P)
        for part in range(2):
            quantize_cov(last, P * part, P * (part + 1))
            project(HALF_TILES + 2 + part, [2])
        store(HALF_TILES + 2)
        store(HALF_TILES + 3, on_vector=True)
